import numpy as np
import ml_dtypes


def mxq(x, axis, fmt="e4m3"):
    dtype, down = {"e4m3": (ml_dtypes.float8_e4m3fn, 7), "e5m2": (ml_dtypes.float8_e5m2, 14)}[fmt]
    v = np.moveaxis(np.asarray(x, np.float32).astype(ml_dtypes.bfloat16).astype(np.float64), axis, -1)
    blocks = v.reshape(v.shape[:-1] + (-1, 32))
    amax = np.abs(blocks).max(-1, keepdims=True)
    byte = np.maximum(np.where(amax > 0, np.frexp(amax)[1] - 1 + 127, 0) - down, 1)
    scale = np.exp2(byte - 127.0)
    codes = (blocks / scale).astype(np.float32).astype(dtype).astype(np.float64)
    return np.moveaxis((codes * scale).reshape(v.shape), -1, axis)


WIDE = False


def mx_kscale(k):
    if not WIDE:
        return np.ones(k)
    levels = np.array([10, -10, 5, -5, 0])
    if k % 512:
        return np.exp2(np.random.permutation(np.resize(levels, k // 32))).repeat(32)
    a = np.empty((k // 512, 16))
    for p in range(k // 512):
        a[p, :8] = np.random.permutation(np.resize(levels, 8))
        for g in range(8):
            far = levels[np.abs(levels - a[p, g]) >= 10]
            a[p, g + 8] = far[np.random.randint(len(far))]
    return np.exp2(a.ravel()).repeat(32)


def f64(x):
    return np.asarray(x).astype(np.float64)


def striped(idx):
    return np.tile(idx.reshape(-1, 16).T, (8, 1)).astype(np.uint16)


def unstriped(offs):
    return offs[:16].T.reshape(-1).astype(np.int64)


E2M1 = np.array([0.0, 0.5, 1.0, 1.5, 2.0, 3.0, 4.0, 6.0, -0.0, -0.5, -1.0, -1.5, -2.0, -3.0, -4.0, -6.0])


def pack_weight(w, fmt):
    k, n = w.shape
    w = f64(np.asarray(w, np.float32).astype(ml_dtypes.bfloat16)).reshape(k // 32, 32, n)
    amax = np.abs(w).max(1)
    if fmt == "e4m3":
        byte = np.frexp(amax)[1] - 1 + 127 - 7
    else:
        mant, ex = np.frexp(amax / 6.0)
        byte = np.where(mant > 0.5, ex, ex - 1) + 127
    byte = np.clip(np.where(amax > 0, byte, 1), 1, 254)
    scaled = (w * np.exp2(127.0 - byte)[:, None, :]).reshape(k, n).astype(np.float32)
    by_word = np.ascontiguousarray(scaled.reshape(k // 512, 128, 4, n).transpose(0, 1, 3, 2))
    if fmt == "e4m3":
        words = by_word.astype(ml_dtypes.float8_e4m3fn).view(np.uint8)
    else:
        c = by_word.astype(ml_dtypes.float4_e2m1fn).view(np.uint8) & 0xF
        words = (c[..., 0::2] | (c[..., 1::2] << 4)).reshape(k // 512, 128, 2 * n)
    return np.ascontiguousarray(words), np.ascontiguousarray(byte.astype(np.uint8).reshape(k // 512, 16, n))


def unpack_weight(words, scales, fmt):
    g, _, n = scales.shape
    words = np.ascontiguousarray(words).reshape(g, 128, n, -1)
    if fmt == "e4m3":
        vals = words.view(ml_dtypes.float8_e4m3fn).astype(np.float64)
    else:
        nib = np.empty((g, 128, n, 4), np.uint8)
        nib[..., 0::2] = words & 0xF
        nib[..., 1::2] = words >> 4
        vals = E2M1[nib]
    vals = vals * np.repeat(np.exp2(scales.astype(np.float64) - 127.0), 8, axis=1)[..., None]
    return vals.transpose(0, 1, 3, 2).reshape(g * 512, n)


def gelu(v):
    return 0.5 * v * (1.0 + np.tanh(np.sqrt(2.0 / np.pi) * (v + 0.044715 * v**3)))


K, T, S, T2, H, N = 1536, 2048, 512, 1024, 1024, 768

def setup_inputs():
    n = np.random.standard_normal
    s = mx_kscale(K)[:, None]
    u = mx_kscale(H)[:, None]
    tab_words, tab_scales = pack_weight(n((K, T)) * s, "e4m3")
    wsup_words, wsup_scales = pack_weight(0.8 * n((K, H)) / np.sqrt(K) / s, "e2m1")
    wdis_words, wdis_scales = pack_weight(n((H, N)) / np.sqrt(H) / u, "e4m3")
    return {
        "tab_words": tab_words, "tab_scales": tab_scales,
        "offs": striped(np.random.permutation(T)[:S]),
        "offs2": striped(np.random.permutation(T2)[:S]),
        "offs3": striped(np.random.permutation(T2)[:S]),
        "wsup_words": wsup_words, "wsup_scales": wsup_scales,
        "wdem": (0.8 * n((K, H)) / np.sqrt(K) / s).astype(np.float32),
        "wg1": np.exp(0.3 * n((128, S))).astype(np.float32),
        "wg2": np.exp(0.3 * n((128, S))).astype(np.float32),
        "stand": (0.7 * n((H, T2))).astype(np.float32),
        "gain": (np.random.uniform(0.5, 2.0, H) * u[:, 0]).astype(np.float32),
        "wdis_words": wdis_words, "wdis_scales": wdis_scales,
    }

def reference(tab_words, tab_scales, offs, offs2, offs3, wsup_words, wsup_scales, wdem,
              wg1, wg2, stand, gain, wdis_words, wdis_scales):
    v = unpack_weight(tab_words, tab_scales, "e4m3")[:, unstriped(offs)]
    wsup = unpack_weight(wsup_words, wsup_scales, "e2m1")
    wdis = unpack_weight(wdis_words, wdis_scales, "e4m3")
    h1 = wsup.T @ v
    h2 = mxq(f64(wdem), 0, "e4m3").T @ v
    sup = np.zeros((H, T2))
    sup[:, unstriped(offs2)] = np.tile(f64(wg1), (H // 128, 1)) * h1
    dem = np.zeros((H, T2))
    dem[:, unstriped(offs3)] = np.tile(f64(wg2), (H // 128, 1)) * h2
    z = np.tanh(sup - dem + f64(stand)) * f64(gain)[:, None]
    return wdis.T @ mxq(z, 0, "e4m3")

@@ -1,0 +1,307 @@
+from contextlib import ExitStack
+
+import concourse.mybir as mybir
+from concourse.masks import make_identity
+
+K, T, S, T2, H, N = 1536, 2048, 512, 1024, 1024, 768
+FLOPS = 2 * K * H * S * 2 + 2 * H * N * T2
+
+F32 = mybir.dt.float32
+BF16 = mybir.dt.bfloat16
+I32 = mybir.dt.int32
+U32 = mybir.dt.uint32
+U16 = mybir.dt.uint16
+U8 = mybir.dt.uint8
+FP8X4 = mybir.dt.float8_e4m3fn_x4
+FP4X4 = mybir.dt.float4_e2m1fn_x4
+MULT = mybir.AluOpType.mult
+ACT = mybir.ActivationFunctionType
+
+P = 128
+PACK = 4
+K_PASS = P * PACK
+K_PASSES = K // K_PASS
+R_PASSES = H // K_PASS
+R_TILES = H // P
+BANK = 512
+M_BLOCKS = T2 // P
+BLOCKS_PER_BANK = BANK // P
+EARLY_TILES = 3
+SUP_PAGES = 4
+DEM_PAGES = 2
+CHUNK = 256
+N_PER_BANK = BANK // CHUNK
+
+
+def tile_list_surplus_exchange_slots_kernel(
+    tc, tab_words, tab_scales, offs, offs2, offs3, wsup_words, wsup_scales, wdem,
+    wg1, wg2, stand, gain, wdis_words, wdis_scales, out,
+):
+    nc = tc.nc
+    with ExitStack() as ctx:
+        keep = ctx.enter_context(tc.tile_pool(name="keep", bufs=1))
+        ring = ctx.enter_context(tc.tile_pool(name="ring", bufs=1))
+        psum = ctx.enter_context(tc.psum_pool(name="psum", bufs=1))
+
+        def load_list(source, name):
+            tile = keep.tile([P, S // 16], U16, name=name)
+            nc.sync.dma_start(tile[:], source)
+            return tile
+
+        def zeroed_plane(width, name, engine=nc.vector):
+            plane = keep.tile([P, width], U8, name=name, align_bytes=64)
+            engine.memset(plane[:].bitcast(I32), 0)
+            return plane
+
+        def load_scale_rows(plane, source, cols, queue=nc.sync):
+            passes = source.shape[0]
+            for quad in range(4):
+                queue.dma_start(
+                    plane[32 * quad : 32 * quad + 4, :].rearrange("r (a c) -> r a c", a=passes).bitcast(I32),
+                    source[:, 4 * quad : 4 * quad + 4, cols].rearrange("a r c -> r a c").bitcast(I32),
+                )
+
+        def big_tile(shape, dtype, name):
+            return ring.tile(shape, dtype, name=name, tag="big", bufs=7, align_bytes=64)
+
+        early_cols = EARLY_TILES * P
+        late_cols = H - early_cols
+        tab_plane = keep.tile([P, K_PASSES * T], U8, name="tab_plane", align_bytes=64)
+        nc.gpsimd.memset(tab_plane[:, : K_PASSES * T // 2].bitcast(I32), 0)
+        nc.vector.memset(tab_plane[:, K_PASSES * T // 2 :].bitcast(I32), 0)
+        wsup_plane_early = zeroed_plane(K_PASSES * early_cols, "wsup_plane_early", nc.gpsimd)
+        wsup_plane_late = zeroed_plane(K_PASSES * late_cols, "wsup_plane_late")
+        wdis_plane = zeroed_plane(R_PASSES * N, "wdis_plane")
+
+        ident = keep.tile([P, P], F32, name="ident")
+        sup_pages = [keep.tile([P, T2], F32, name=f"sup_page{i}") for i in range(SUP_PAGES)]
+        dem_pages = [keep.tile([P, T2], F32, name=f"dem_page{i}") for i in range(DEM_PAGES)]
+        for page in sup_pages + dem_pages:
+            nc.gpsimd.memset(page[:], 0.0)
+        make_identity(nc, ident[:])
+
+        lot_list = load_list(offs, "lot_list")
+        tab_tiles = []
+
+        def load_tab(a):
+            tile = big_tile([P, T], U32, f"tab{a}")
+            nc.sync.dma_start(tile[:].bitcast(I32), tab_words[a].rearrange("p t i -> p (t i)").bitcast(I32))
+            tab_tiles.append(tile)
+
+        def load_wsup(c0, c1, name):
+            tile = keep.tile([P, K_PASSES, 2 * (c1 - c0)], U8, name=name, align_bytes=64)
+            nc.sync.dma_start(
+                tile[:].bitcast(I32), wsup_words.rearrange("a p c -> p a c")[:, :, 2 * c0 : 2 * c1].bitcast(I32)
+            )
+            return tile
+
+        load_tab(0)
+        load_scale_rows(tab_plane, tab_scales, slice(0, T), nc.scalar)
+        load_tab(1)
+        load_tab(2)
+        load_scale_rows(wsup_plane_early, wsup_scales, slice(0, early_cols))
+        wsup_early = load_wsup(0, early_cols, "wsup_early")
+        wg1_sb = keep.tile([P, S], F32, name="wg1_sb")
+        nc.sync.dma_start(wg1_sb[:], wg1)
+        sup_list = load_list(offs2, "sup_list")
+
+        lot_planes = []
+        lot_words = []
+        for a in range(K_PASSES):
+            plane = keep.tile([P, S], U8, name=f"lot_plane{a}", align_bytes=64)
+            nc.vector.tensor_copy(plane[:], tab_plane[:, a * T : (a + 1) * T].indirect(lot_list[:]))
+            lot_planes.append(plane)
+            words = keep.tile([P, S], U32, name=f"lot_words{a}", align_bytes=64)
+            nc.vector.tensor_copy(words[:], tab_tiles[a][:].indirect(lot_list[:]))
+            lot_words.append(words)
+
+        def score_tile():
+            return ring.tile([P, S], F32, name="scores", tag="scores", bufs=12)
+
+        def supply(i, words, plane, first_tile, width):
+            c0 = (i - first_tile) * P
+            acc = psum.tile([P, BANK], F32, name="acc", tag="acc", bufs=3)
+            for a in range(K_PASSES):
+                nc.tensor.matmul_mx(
+                    out=acc[:],
+                    lhsT=words[:, a, 2 * c0 : 2 * (c0 + P)].bitcast(FP4X4),
+                    lhsT_scale=plane[:, a * width + c0 : a * width + c0 + P],
+                    rhs=lot_words[a][:].bitcast(FP8X4),
+                    rhs_scale=lot_planes[a][:],
+                    start=(a == 0),
+                    stop=(a == K_PASSES - 1),
+                )
+            h1 = score_tile()
+            nc.scalar.copy(h1[:], acc[:])
+            page = sup_pages[i % SUP_PAGES]
+            nc.vector.tensor_tensor(page[:].indirect(sup_list[:]), h1[:], wg1_sb[:], MULT)
+
+        wdem_codes = {}
+        wdem_planes = {}
+
+        def quantize_wdem(half):
+            cols = slice(half * BANK, (half + 1) * BANK)
+            for a in range(K_PASSES):
+                raw = big_tile([P, PACK, BANK], F32, f"wdem_raw{half}{a}")
+                nc.sync.dma_start(
+                    raw[:], wdem[a * K_PASS : (a + 1) * K_PASS, cols].rearrange("(p j) c -> p j c", j=PACK)
+                )
+                woven = ring.tile([P, BANK, PACK], BF16, name="woven", tag="woven", bufs=4, align_bytes=64)
+                nc.scalar.copy(
+                    woven[:].rearrange("p (c i) j -> p c j i", i=4),
+                    raw[:].rearrange("p j (c i) -> p c j i", i=4),
+                )
+                codes = keep.tile([P, BANK], U32, name=f"wdem_codes{half}{a}", align_bytes=64)
+                plane = keep.tile([P, BANK], U8, name=f"wdem_plane{half}{a}", align_bytes=64)
+                nc.vector.quantize_mx(
+                    out=codes[:].bitcast(FP8X4), scales=plane[:], in_=woven[:].rearrange("p c j -> p (c j)")
+                )
+                wdem_codes[half, a] = codes
+                wdem_planes[half, a] = plane
+
+        def demand(i):
+            half, c0 = divmod(i * P, BANK)
+            acc = psum.tile([P, BANK], F32, name="acc", tag="acc", bufs=3)
+            for a in range(K_PASSES):
+                nc.tensor.matmul_mx(
+                    out=acc[:],
+                    lhsT=wdem_codes[half, a][:, c0 : c0 + P].bitcast(FP8X4),
+                    lhsT_scale=wdem_planes[half, a][:, c0 : c0 + P],
+                    rhs=lot_words[a][:].bitcast(FP8X4),
+                    rhs_scale=lot_planes[a][:],
+                    start=(a == 0),
+                    stop=(a == K_PASSES - 1),
+                )
+            h2 = score_tile()
+            nc.scalar.activation(h2[:], acc[:], ACT.Copy, scale=-1.0)
+            page = dem_pages[i % DEM_PAGES]
+            nc.vector.tensor_tensor(page[:].indirect(dem_list[:]), h2[:], wg2_sb[:], MULT)
+
+        bounded = {}
+
+        def imbalance(i):
+            a, quad = divmod(i, 4)
+            standing = ring.tile([P, T2], F32, name="standing", tag="standing", bufs=4)
+            nc.sync.dma_start(standing[:], stand[i * P : (i + 1) * P, :])
+            terms = [standing, sup_pages[i % SUP_PAGES], dem_pages[i % DEM_PAGES]]
+            for half in range(T2 // BANK):
+                if quad == 0:
+                    bounded[a, half] = big_tile([P, BLOCKS_PER_BANK, PACK, P], F32, f"bounded{a}{half}")
+                total = psum.tile([P, BLOCKS_PER_BANK, P], F32, name="total", tag="total", bufs=2)
+                for n_term, term in enumerate(terms):
+                    for b in range(BLOCKS_PER_BANK):
+                        m0 = half * BANK + b * P
+                        nc.tensor.matmul(
+                            total[:, b, :], term[:, m0 : m0 + P], ident[:], is_transpose=True,
+                            start=(n_term == 0 and b == 0),
+                            stop=(n_term == len(terms) - 1 and b == BLOCKS_PER_BANK - 1),
+                        )
+                nc.scalar.activation(
+                    bounded[a, half][:, :, :, 32 * quad : 32 * (quad + 1)],
+                    total[:].rearrange("m b (q t) -> m b t q", t=PACK),
+                    ACT.Tanh,
+                )
+
+        for i in range(EARLY_TILES):
+            supply(i, wsup_early, wsup_plane_early, 0, early_cols)
+        quantize_wdem(0)
+        wg2_sb = keep.tile([P, S], F32, name="wg2_sb")
+        nc.sync.dma_start(wg2_sb[:], wg2)
+        dem_list = load_list(offs3, "dem_list")
+        wsup_late = load_wsup(early_cols, H, "wsup_late")
+        load_scale_rows(wsup_plane_late, wsup_scales, slice(early_cols, H))
+        supply(3, wsup_late, wsup_plane_late, EARLY_TILES, late_cols)
+        demand(0)
+        demand(1)
+        quantize_wdem(1)
+
+        gain_sb = keep.tile([P, R_PASSES, PACK], F32, name="gain_sb")
+        nc.sync.dma_start(gain_sb[:], gain.rearrange("(a p t) -> p a t", p=P, t=PACK))
+        wdis_sb = keep.tile([P, R_PASSES, N], U32, name="wdis_sb", align_bytes=64)
+
+        z_codes = {}
+        z_planes = {}
+
+        def quantize_z(a, m0, width, woven):
+            codes = keep.tile([P, width], U32, name=f"z_codes{a}_{m0}", align_bytes=64)
+            plane = keep.tile([P, width], U8, name=f"z_plane{a}_{m0}", align_bytes=64)
+            nc.vector.quantize_mx(
+                out=codes[:].bitcast(FP8X4), scales=plane[:], in_=woven[:].rearrange("p m t -> p (m t)")
+            )
+            for c0 in range(0, width, CHUNK):
+                z_codes[a, m0 + c0] = codes[:, c0 : c0 + CHUNK]
+                z_planes[a, m0 + c0] = plane[:, c0 : c0 + CHUNK]
+
+        def z_on_scalar(a, half):
+            rows = ring.tile([P, PACK, BANK], BF16, name="z_rows", tag="woven", bufs=4, align_bytes=64)
+            for t in range(PACK):
+                back = psum.tile([P, BLOCKS_PER_BANK, P], F32, name="back", tag="back", bufs=3)
+                for b in range(BLOCKS_PER_BANK):
+                    nc.tensor.transpose(back[:, b, :], bounded[a, half][:, b, t, :], ident[:])
+                nc.scalar.activation(
+                    rows[:, t, :], back[:].rearrange("p b m -> p (b m)"), ACT.Copy, scale=gain_sb[:, a, t : t + 1]
+                )
+            woven = ring.tile([P, BANK, PACK], BF16, name="woven", tag="woven", bufs=4, align_bytes=64)
+            nc.scalar.copy(
+                woven[:].rearrange("p (c i) t -> p c t i", i=4),
+                rows[:].rearrange("p t (c i) -> p c t i", i=4),
+            )
+            quantize_z(a, half * BANK, BANK, woven)
+
+        def z_on_vector(a, m0):
+            woven = ring.tile([P, CHUNK, PACK], BF16, name="woven", tag="woven", bufs=4, align_bytes=64)
+            for mb in range(m0 // P, (m0 + CHUNK) // P):
+                half, b = divmod(mb, BLOCKS_PER_BANK)
+                back = psum.tile([P, PACK, P], F32, name="back", tag="back", bufs=3)
+                for t in range(PACK):
+                    nc.tensor.transpose(back[:, t, :], bounded[a, half][:, b, t, :], ident[:])
+                c0 = mb * P - m0
+                nc.vector.tensor_tensor(
+                    woven[:, c0 : c0 + P, :],
+                    back[:].rearrange("p t m -> p m t"),
+                    gain_sb[:, a, :].unsqueeze(1).to_broadcast([P, P, PACK]),
+                    MULT,
+                )
+            quantize_z(a, m0, CHUNK, woven)
+
+        for i in range(R_TILES):
+            imbalance(i)
+            if i == 0:
+                nc.sync.dma_start(
+                    wdis_sb[:].bitcast(I32), wdis_words.rearrange("a p c i -> p a (c i)").bitcast(I32)
+                )
+                load_scale_rows(wdis_plane, wdis_scales, slice(0, N))
+            if i + SUP_PAGES < R_TILES:
+                supply(i + SUP_PAGES, wsup_late, wsup_plane_late, EARLY_TILES, late_cols)
+            if i + DEM_PAGES < R_TILES:
+                demand(i + DEM_PAGES)
+            if i == 3:
+                for half in range(T2 // BANK):
+                    z_on_scalar(0, half)
+
+        out_rows = out.rearrange("(j p) m -> p j m", p=P)
+        n_banks = N // P // N_PER_BANK
+        for m0 in range(0, T2, CHUNK):
+            z_on_vector(1, m0)
+            for bank in range(n_banks):
+                acc = psum.tile([P, N_PER_BANK, CHUNK], F32, name="acc", tag="acc", bufs=3)
+                for a in range(R_PASSES):
+                    for jj in range(N_PER_BANK):
+                        n0 = (bank * N_PER_BANK + jj) * P
+                        nc.tensor.matmul_mx(
+                            out=acc[:, jj, :],
+                            lhsT=wdis_sb[:, a, n0 : n0 + P].bitcast(FP8X4),
+                            lhsT_scale=wdis_plane[:, a * N + n0 : a * N + n0 + P],
+                            rhs=z_codes[a, m0].bitcast(FP8X4),
+                            rhs_scale=z_planes[a, m0],
+                            start=(a == 0 and jj == 0),
+                            stop=(a == R_PASSES - 1 and jj == N_PER_BANK - 1),
+                        )
+                result = ring.tile([P, N_PER_BANK, CHUNK], F32, name="result", tag="scores", bufs=12)
+                if m0 == T2 - CHUNK and bank != 1:
+                    nc.vector.tensor_copy(result[:], acc[:])
+                else:
+                    nc.scalar.copy(result[:], acc[:])
+                nc.sync.dma_start(
+                    out_rows[:, bank * N_PER_BANK : (bank + 1) * N_PER_BANK, m0 : m0 + CHUNK], result[:]
+                )

@@ -15,6 +15,7 @@ U8 = mybir.dt.uint8
 FP8X4 = mybir.dt.float8_e4m3fn_x4
 FP4X4 = mybir.dt.float4_e2m1fn_x4
 MULT = mybir.AluOpType.mult
+ADD = mybir.AluOpType.add
 ACT = mybir.ActivationFunctionType
 
 P = 128
@@ -26,11 +27,13 @@ R_TILES = H // P
 BANK = 512
 M_BLOCKS = T2 // P
 BLOCKS_PER_BANK = BANK // P
-EARLY_TILES = 3
-SUP_PAGES = 4
-DEM_PAGES = 2
-CHUNK = 256
-N_PER_BANK = BANK // CHUNK
+EARLY_TILES = 1
+PAGES = 3
+TAB_BYTES = 4 * T
+PAGE_BYTES = 4 * T2
+QUARTER = 256
+EARLY_GROUPS = 6
+CHUNKS = ((0, 128), (128, 128), (256, 256), (512, 256), (768, 256))
 
 
 def tile_list_surplus_exchange_slots_kernel(
@@ -41,6 +44,7 @@ def tile_list_surplus_exchange_slots_kernel(
     with ExitStack() as ctx:
         keep = ctx.enter_context(tc.tile_pool(name="keep", bufs=1))
         ring = ctx.enter_context(tc.tile_pool(name="ring", bufs=1))
+        shared = ctx.enter_context(tc.tile_pool(name="shared", bufs=1))
         psum = ctx.enter_context(tc.psum_pool(name="psum", bufs=1))
 
         def load_list(source, name):
@@ -48,7 +52,7 @@ def tile_list_surplus_exchange_slots_kernel(
             nc.sync.dma_start(tile[:], source)
             return tile
 
-        def zeroed_plane(width, name, engine=nc.vector):
+        def zeroed_plane(width, name, engine):
             plane = keep.tile([P, width], U8, name=name, align_bytes=64)
             engine.memset(plane[:].bitcast(I32), 0)
             return plane
@@ -62,48 +66,44 @@ def tile_list_surplus_exchange_slots_kernel(
                 )
 
         def big_tile(shape, dtype, name):
-            return ring.tile(shape, dtype, name=name, tag="big", bufs=7, align_bytes=64)
+            return ring.tile(shape, dtype, name=name, tag="big", bufs=5, align_bytes=64)
 
         early_cols = EARLY_TILES * P
         late_cols = H - early_cols
-        tab_plane = keep.tile([P, K_PASSES * T], U8, name="tab_plane", align_bytes=64)
-        nc.gpsimd.memset(tab_plane[:, : K_PASSES * T // 2].bitcast(I32), 0)
-        nc.vector.memset(tab_plane[:, K_PASSES * T // 2 :].bitcast(I32), 0)
-        wsup_plane_early = zeroed_plane(K_PASSES * early_cols, "wsup_plane_early", nc.gpsimd)
-        wsup_plane_late = zeroed_plane(K_PASSES * late_cols, "wsup_plane_late")
-        wdis_plane = zeroed_plane(R_PASSES * N, "wdis_plane")
+        tab_plane = zeroed_plane(K_PASSES * T, "tab_plane", nc.gpsimd)
+        wsup_plane_late = zeroed_plane(K_PASSES * late_cols, "wsup_plane_late", nc.vector)
+        wdis_plane = zeroed_plane(R_PASSES * N, "wdis_plane", nc.vector)
+        sup_pages = [keep.tile([P, T2], F32, name=f"sup_page{i}") for i in range(PAGES)]
+        for page in sup_pages:
+            nc.vector.memset(page[:].bitcast(I32), 0)
+        wsup_plane_early = zeroed_plane(K_PASSES * early_cols, "wsup_plane_early", nc.vector)
 
-        ident = keep.tile([P, P], F32, name="ident")
-        sup_pages = [keep.tile([P, T2], F32, name=f"sup_page{i}") for i in range(SUP_PAGES)]
-        dem_pages = [keep.tile([P, T2], F32, name=f"dem_page{i}") for i in range(DEM_PAGES)]
-        for page in sup_pages + dem_pages:
-            nc.gpsimd.memset(page[:], 0.0)
-        make_identity(nc, ident[:])
-
-        lot_list = load_list(offs, "lot_list")
         tab_tiles = []
 
         def load_tab(a):
-            tile = big_tile([P, T], U32, f"tab{a}")
+            tile = shared.tile([P, T], U32, name=f"tab{a}", offset=a * TAB_BYTES, align_bytes=64)
             nc.sync.dma_start(tile[:].bitcast(I32), tab_words[a].rearrange("p t i -> p (t i)").bitcast(I32))
             tab_tiles.append(tile)
 
-        def load_wsup(c0, c1, name):
+        def load_wsup(c0, c1, name, queue):
             tile = keep.tile([P, K_PASSES, 2 * (c1 - c0)], U8, name=name, align_bytes=64)
-            nc.sync.dma_start(
+            queue.dma_start(
                 tile[:].bitcast(I32), wsup_words.rearrange("a p c -> p a c")[:, :, 2 * c0 : 2 * c1].bitcast(I32)
             )
             return tile
 
         load_tab(0)
-        load_scale_rows(tab_plane, tab_scales, slice(0, T), nc.scalar)
+        lot_list = load_list(offs, "lot_list")
+        sup_list = load_list(offs2, "sup_list")
+        load_scale_rows(tab_plane, tab_scales, slice(0, T))
         load_tab(1)
         load_tab(2)
-        load_scale_rows(wsup_plane_early, wsup_scales, slice(0, early_cols))
-        wsup_early = load_wsup(0, early_cols, "wsup_early")
+        load_scale_rows(wsup_plane_early, wsup_scales, slice(0, early_cols), nc.scalar)
+        wsup_early = load_wsup(0, early_cols, "wsup_early", nc.scalar)
         wg1_sb = keep.tile([P, S], F32, name="wg1_sb")
         nc.sync.dma_start(wg1_sb[:], wg1)
-        sup_list = load_list(offs2, "sup_list")
+        load_scale_rows(wsup_plane_late, wsup_scales, slice(early_cols, H))
+        wsup_mid = load_wsup(early_cols, K_PASS, "wsup_mid", nc.sync)
 
         lot_planes = []
         lot_words = []
@@ -115,12 +115,36 @@ def tile_list_surplus_exchange_slots_kernel(
             nc.vector.tensor_copy(words[:], tab_tiles[a][:].indirect(lot_list[:]))
             lot_words.append(words)
 
-        def score_tile():
-            return ring.tile([P, S], F32, name="scores", tag="scores", bufs=12)
+        spot = 2 * TAB_BYTES - PAGE_BYTES // 2
+        dem_pages = []
 
-        def supply(i, words, plane, first_tile, width):
+        def zeroed_page(name, offset):
+            page = shared.tile([P, T2], F32, name=name, offset=offset)
+            nc.gpsimd.memset(page[:], 0.0)
+            dem_pages.append(page)
+
+        zeroed_page("dem_page0", spot)
+        zeroed_page("dem_page1", spot + PAGE_BYTES)
+        spot = spot + 2 * PAGE_BYTES
+        ident = shared.tile([P, P], F32, name="ident", offset=spot)
+        make_identity(nc, ident[:])
+        zeroed_page("dem_page2", spot + 4 * P)
+
+
+        banks = [psum.tile([P, BANK], F32, name=f"bank{i}") for i in range(8)]
+        pairs = (banks[3:5], banks[5:7])
+        acc_turn = []
+
+        def next_acc():
+            acc_turn.append(None)
+            return banks[(len(acc_turn) - 1) % 3]
+
+        def score_tile():
+            return ring.tile([P, S], F32, name="scores", tag="scores", bufs=10)
+
+        def supply(i, words, plane, first_tile, width, h1):
             c0 = (i - first_tile) * P
-            acc = psum.tile([P, BANK], F32, name="acc", tag="acc", bufs=3)
+            acc = next_acc()
             for a in range(K_PASSES):
                 nc.tensor.matmul_mx(
                     out=acc[:],
@@ -131,13 +155,37 @@ def tile_list_surplus_exchange_slots_kernel(
                     start=(a == 0),
                     stop=(a == K_PASSES - 1),
                 )
+            nc.scalar.copy(h1, acc[:])
+            return h1
+
+        def supply_turned(words, plane, c0, width):
+            turned = raws[3][:].rearrange("p j (t q) -> p j t q", t=PACK)
+            for jb in range(S // P):
+                acc = next_acc()
+                for a in range(K_PASSES):
+                    nc.tensor.matmul_mx(
+                        out=acc[:],
+                        lhsT=lot_words[a][:, jb * P : (jb + 1) * P].bitcast(FP8X4),
+                        lhsT_scale=lot_planes[a][:, jb * P : (jb + 1) * P],
+                        rhs=words[:, a, :].bitcast(FP4X4),
+                        rhs_scale=plane[:, a * width + c0 : a * width + c0 + BANK],
+                        start=(a == 0),
+                        stop=(a == K_PASSES - 1),
+                    )
+                nc.scalar.copy(turned[:, jb], acc[:].rearrange("j (p t) -> j t p", t=PACK))
+            return turned
+
+        def supply_plane(turned, t):
+            acc = next_acc()
+            for jb in range(S // P):
+                nc.tensor.transpose(acc[:, jb * P : (jb + 1) * P], turned[:, jb, t, :], ident[:])
             h1 = score_tile()
             nc.scalar.copy(h1[:], acc[:])
-            page = sup_pages[i % SUP_PAGES]
-            nc.vector.tensor_tensor(page[:].indirect(sup_list[:]), h1[:], wg1_sb[:], MULT)
+            return h1[:]
 
         wdem_codes = {}
         wdem_planes = {}
+        raws = []
 
         def quantize_wdem(half):
             cols = slice(half * BANK, (half + 1) * BANK)
@@ -147,10 +195,16 @@ def tile_list_surplus_exchange_slots_kernel(
                     raw[:], wdem[a * K_PASS : (a + 1) * K_PASS, cols].rearrange("(p j) c -> p j c", j=PACK)
                 )
                 woven = ring.tile([P, BANK, PACK], BF16, name="woven", tag="woven", bufs=4, align_bytes=64)
-                nc.scalar.copy(
-                    woven[:].rearrange("p (c i) j -> p c j i", i=4),
-                    raw[:].rearrange("p j (c i) -> p c j i", i=4),
-                )
+                if half == 0:
+                    nc.scalar.copy(
+                        woven[:].rearrange("p (c i) j -> p c j i", i=4),
+                        raw[:].rearrange("p j (c i) -> p c j i", i=4),
+                    )
+                else:
+                    nc.scalar.copy(
+                        woven[:].rearrange("p (t q) j -> p q j t", t=PACK),
+                        raw[:].rearrange("p j (q t) -> p q j t", t=PACK),
+                    )
                 codes = keep.tile([P, BANK], U32, name=f"wdem_codes{half}{a}", align_bytes=64)
                 plane = keep.tile([P, BANK], U8, name=f"wdem_plane{half}{a}", align_bytes=64)
                 nc.vector.quantize_mx(
@@ -158,10 +212,12 @@ def tile_list_surplus_exchange_slots_kernel(
                 )
                 wdem_codes[half, a] = codes
                 wdem_planes[half, a] = plane
+                raws.append(raw)
+            return raw
 
-        def demand(i):
+        def demand(i, h2):
             half, c0 = divmod(i * P, BANK)
-            acc = psum.tile([P, BANK], F32, name="acc", tag="acc", bufs=3)
+            acc = next_acc()
             for a in range(K_PASSES):
                 nc.tensor.matmul_mx(
                     out=acc[:],
@@ -172,52 +228,39 @@ def tile_list_surplus_exchange_slots_kernel(
                     start=(a == 0),
                     stop=(a == K_PASSES - 1),
                 )
-            h2 = score_tile()
-            nc.scalar.activation(h2[:], acc[:], ACT.Copy, scale=-1.0)
-            page = dem_pages[i % DEM_PAGES]
-            nc.vector.tensor_tensor(page[:].indirect(dem_list[:]), h2[:], wg2_sb[:], MULT)
+            nc.scalar.activation(h2, acc[:], ACT.Copy, scale=-1.0)
+            return h2
 
-        bounded = {}
+        def place(page, slots, scores, weights):
+            nc.vector.tensor_tensor(page[:].indirect(slots[:]), scores, weights, MULT)
 
-        def imbalance(i):
-            a, quad = divmod(i, 4)
+        def load_standing(rows):
             standing = ring.tile([P, T2], F32, name="standing", tag="standing", bufs=4)
-            nc.sync.dma_start(standing[:], stand[i * P : (i + 1) * P, :])
-            terms = [standing, sup_pages[i % SUP_PAGES], dem_pages[i % DEM_PAGES]]
-            for half in range(T2 // BANK):
-                if quad == 0:
-                    bounded[a, half] = big_tile([P, BLOCKS_PER_BANK, PACK, P], F32, f"bounded{a}{half}")
-                total = psum.tile([P, BLOCKS_PER_BANK, P], F32, name="total", tag="total", bufs=2)
-                for n_term, term in enumerate(terms):
+            nc.sync.dma_start(standing[:], rows)
+            return standing
+
+        def add_turned(terms, total_banks):
+            for n_term, term in enumerate(terms):
+                for half in range(T2 // BANK):
                     for b in range(BLOCKS_PER_BANK):
                         m0 = half * BANK + b * P
                         nc.tensor.matmul(
-                            total[:, b, :], term[:, m0 : m0 + P], ident[:], is_transpose=True,
+                            total_banks[half][:, b * P : (b + 1) * P], term[:, m0 : m0 + P], ident[:],
+                            is_transpose=True,
                             start=(n_term == 0 and b == 0),
                             stop=(n_term == len(terms) - 1 and b == BLOCKS_PER_BANK - 1),
                         )
-                nc.scalar.activation(
-                    bounded[a, half][:, :, :, 32 * quad : 32 * (quad + 1)],
-                    total[:].rearrange("m b (q t) -> m b t q", t=PACK),
-                    ACT.Tanh,
-                )
 
-        for i in range(EARLY_TILES):
-            supply(i, wsup_early, wsup_plane_early, 0, early_cols)
-        quantize_wdem(0)
-        wg2_sb = keep.tile([P, S], F32, name="wg2_sb")
-        nc.sync.dma_start(wg2_sb[:], wg2)
-        dem_list = load_list(offs3, "dem_list")
-        wsup_late = load_wsup(early_cols, H, "wsup_late")
-        load_scale_rows(wsup_plane_late, wsup_scales, slice(early_cols, H))
-        supply(3, wsup_late, wsup_plane_late, EARLY_TILES, late_cols)
-        demand(0)
-        demand(1)
-        quantize_wdem(1)
+        def turn_back(total, func, targets):
+            turned = ring.tile([P, BANK], F32, name="turned_sum", tag="turned_sum", bufs=3)
+            nc.scalar.activation(turned[:], total[:], func)
+            for b in range(BLOCKS_PER_BANK):
+                nc.tensor.transpose(targets[b], turned[:, b * P : (b + 1) * P], ident[:])
 
-        gain_sb = keep.tile([P, R_PASSES, PACK], F32, name="gain_sb")
-        nc.sync.dma_start(gain_sb[:], gain.rearrange("(a p t) -> p a t", p=P, t=PACK))
-        wdis_sb = keep.tile([P, R_PASSES, N], U32, name="wdis_sb", align_bytes=64)
+        def load_dealt(target, source, t):
+            rows = source.rearrange("(q t) j -> q t j", t=PACK)[:, t, :]
+            for rep in range(P // 32):
+                nc.sync.dma_start(target[32 * rep : 32 * (rep + 1)], rows)
 
         z_codes = {}
         z_planes = {}
@@ -228,80 +271,162 @@ def tile_list_surplus_exchange_slots_kernel(
             nc.vector.quantize_mx(
                 out=codes[:].bitcast(FP8X4), scales=plane[:], in_=woven[:].rearrange("p m t -> p (m t)")
             )
-            for c0 in range(0, width, CHUNK):
-                z_codes[a, m0 + c0] = codes[:, c0 : c0 + CHUNK]
-                z_planes[a, m0 + c0] = plane[:, c0 : c0 + CHUNK]
+            for c0, cw in CHUNKS:
+                if m0 <= c0 < m0 + width:
+                    z_codes[a, c0] = codes[:, c0 - m0 : c0 - m0 + cw]
+                    z_planes[a, c0] = plane[:, c0 - m0 : c0 - m0 + cw]
 
-        def z_on_scalar(a, half):
-            rows = ring.tile([P, PACK, BANK], BF16, name="z_rows", tag="woven", bufs=4, align_bytes=64)
-            for t in range(PACK):
-                back = psum.tile([P, BLOCKS_PER_BANK, P], F32, name="back", tag="back", bufs=3)
-                for b in range(BLOCKS_PER_BANK):
-                    nc.tensor.transpose(back[:, b, :], bounded[a, half][:, b, t, :], ident[:])
+        place(sup_pages[0], sup_list, supply(0, wsup_early, wsup_plane_early, 0, early_cols, score_tile()[:]), wg1_sb[:])
+        h1 = supply(1, wsup_mid, wsup_plane_late, EARLY_TILES, late_cols, score_tile()[:])
+        place(sup_pages[1], sup_list, h1, wg1_sb[:])
+        last_raw = quantize_wdem(0)
+        wg2_sb = keep.tile([P, S], F32, name="wg2_sb")
+        nc.sync.dma_start(wg2_sb[:], wg2)
+        dem_list = load_list(offs3, "dem_list")
+        h1 = supply(2, wsup_mid, wsup_plane_late, EARLY_TILES, late_cols, last_raw[:, 0, :])
+        place(sup_pages[2], sup_list, h1, wg1_sb[:])
+        quantize_wdem(1)
+        for i in range(PAGES):
+            place(dem_pages[i], dem_list, demand(i, raws[4][:, i, :]), wg2_sb[:])
+        h1_tile3 = supply(3, wsup_mid, wsup_plane_late, EARLY_TILES, late_cols, raws[5][:, 0, :])
+        h2_tile3 = demand(3, raws[5][:, 1, :])
+        wsup_late = load_wsup(K_PASS, H, "wsup_late", nc.sync)
+        standing = [load_standing(stand[0:P, :])]
+        sup_turned = supply_turned(wsup_late, wsup_plane_late, K_PASS - early_cols, late_cols)
+        h1_planes = [supply_plane(sup_turned, t) for t in range(PACK)]
+        standing.append(load_standing(stand[P : 2 * P, :]))
+        standing.append(load_standing(stand[2 * P : 3 * P, :]))
+        standing.append(load_standing(stand[3 * P : 4 * P, :]))
+        wg1_dealt = [keep.tile([P, S], F32, name=f"wg1_dealt{t}") for t in range(PACK)]
+        wg2_dealt = [keep.tile([P, S], F32, name=f"wg2_dealt{t}") for t in range(PACK - 1)]
+        for t in range(PACK):
+            load_dealt(wg1_dealt[t][:], wg1, t)
+            if t < PACK - 1:
+                load_dealt(wg2_dealt[t][:], wg2, t)
+        gain_sb = keep.tile([P, R_PASSES, PACK], F32, name="gain_sb")
+        nc.sync.dma_start(gain_sb[:], gain.rearrange("(a p t) -> p a t", p=P, t=PACK))
+        wdis_sb = keep.tile([P, R_PASSES, N], U32, name="wdis_sb", align_bytes=64)
+        nc.sync.dma_start(wdis_sb[:].bitcast(I32), wdis_words.rearrange("a p c i -> p a (c i)").bitcast(I32))
+        load_scale_rows(wdis_plane, wdis_scales, slice(0, N))
+
+        stand_planes = stand[K_PASS:, :].rearrange("(p t) m -> p t m", t=PACK)
+        bounded = [big_tile([P, BLOCKS_PER_BANK, PACK, P], F32, f"bounded{half}") for half in range(T2 // BANK)]
+        for i in range(4):
+            total_banks = pairs[i % 2]
+            add_turned([standing[i], sup_pages[i % PAGES], dem_pages[i % PAGES]], total_banks)
+            if i == 1:
+                h2_planes = [demand(4 + t, score_tile()[:]) for t in range(PACK)]
+            if i == 0:
+                place(sup_pages[0], sup_list, h1_tile3, wg1_sb[:])
+                place(dem_pages[0], dem_list, h2_tile3, wg2_sb[:])
+            else:
+                place(sup_pages[i % PAGES], sup_list, h1_planes[i - 1], wg1_dealt[i - 1][:])
+                place(dem_pages[i % PAGES], dem_list, h2_planes[i - 1], wg2_dealt[i - 1][:])
+            for half in range(T2 // BANK):
                 nc.scalar.activation(
-                    rows[:, t, :], back[:].rearrange("p b m -> p (b m)"), ACT.Copy, scale=gain_sb[:, a, t : t + 1]
+                    bounded[half][:, :, :, 32 * i : 32 * (i + 1)],
+                    total_banks[half][:].rearrange("m (b q t) -> m b t q", b=BLOCKS_PER_BANK, t=PACK),
+                    ACT.Tanh,
                 )
+            standing.append(load_standing(stand_planes[:, i, :]))
+
+        z0_banks = [7, 0, 1, 2, 7, 0, 5, 6]
+        z0_rows = []
+        for half in range(T2 // BANK):
+            rows = ring.tile([P, PACK, BANK], BF16, name="z_rows", tag="woven", bufs=4, align_bytes=64)
+            z0_rows.append(rows)
+            for t in range(PACK):
+                back = banks[z0_banks[half * PACK + t]]
+                for b in range(BLOCKS_PER_BANK):
+                    nc.tensor.transpose(back[:, b * P : (b + 1) * P], bounded[half][:, b, t, :], ident[:])
+                nc.scalar.activation(rows[:, t, :], back[:], ACT.Copy, scale=gain_sb[:, 0, t : t + 1])
+        for half in range(T2 // BANK):
+            rows = z0_rows[half]
             woven = ring.tile([P, BANK, PACK], BF16, name="woven", tag="woven", bufs=4, align_bytes=64)
             nc.scalar.copy(
                 woven[:].rearrange("p (c i) t -> p c t i", i=4),
                 rows[:].rearrange("p t (c i) -> p c t i", i=4),
             )
-            quantize_z(a, half * BANK, BANK, woven)
+            quantize_z(0, half * BANK, BANK, woven)
+        wg2_last = z0_rows[1][:].rearrange("p t m -> p (t m)").bitcast(F32)[:, :S]
+        load_dealt(wg2_last, wg2, PACK - 1)
 
-        def z_on_vector(a, m0):
-            woven = ring.tile([P, CHUNK, PACK], BF16, name="woven", tag="woven", bufs=4, align_bytes=64)
-            for mb in range(m0 // P, (m0 + CHUNK) // P):
-                half, b = divmod(mb, BLOCKS_PER_BANK)
-                back = psum.tile([P, PACK, P], F32, name="back", tag="back", bufs=3)
-                for t in range(PACK):
-                    nc.tensor.transpose(back[:, t, :], bounded[a, half][:, b, t, :], ident[:])
-                c0 = mb * P - m0
-                nc.vector.tensor_tensor(
-                    woven[:, c0 : c0 + P, :],
-                    back[:].rearrange("p t m -> p m t"),
-                    gain_sb[:, a, :].unsqueeze(1).to_broadcast([P, P, PACK]),
-                    MULT,
+        z_rows = {m0: keep.tile([P, PACK, width], BF16, name=f"z_rows{m0}") for m0, width in CHUNKS}
+        last = PACK - 1
+        last_pages = (4 + last) % PAGES
+        for t in range(last):
+            total_banks = pairs[t % 2]
+            add_turned([standing[4 + t], sup_pages[(4 + t) % PAGES], dem_pages[(4 + t) % PAGES]], total_banks)
+            if t == 0:
+                place(sup_pages[last_pages], sup_list, h1_planes[last], wg1_dealt[last][:])
+            for half in range(T2 // BANK):
+                if t < last - 1:
+                    back = banks[((1, 2), (7, 0))[t][half]]
+                    quarters = [back[:, :QUARTER], back[:, QUARTER:]]
+                else:
+                    quarters = [banks[b][:, :QUARTER] for b in ((0, 1), (2, 7))[half]]
+                turn_back(
+                    total_banks[half], ACT.Tanh, [quarters[b // 2][:, b % 2 * P : (b % 2 + 1) * P] for b in range(4)]
                 )
-            quantize_z(a, m0, CHUNK, woven)
-
-        for i in range(R_TILES):
-            imbalance(i)
-            if i == 0:
-                nc.sync.dma_start(
-                    wdis_sb[:].bitcast(I32), wdis_words.rearrange("a p c i -> p a (c i)").bitcast(I32)
-                )
-                load_scale_rows(wdis_plane, wdis_scales, slice(0, N))
-            if i + SUP_PAGES < R_TILES:
-                supply(i + SUP_PAGES, wsup_late, wsup_plane_late, EARLY_TILES, late_cols)
-            if i + DEM_PAGES < R_TILES:
-                demand(i + DEM_PAGES)
-            if i == 3:
-                for half in range(T2 // BANK):
-                    z_on_scalar(0, half)
+                for m0, width in CHUNKS:
+                    if m0 // BANK == half:
+                        c0 = m0 % QUARTER
+                        nc.scalar.activation(
+                            z_rows[m0][:, t, :], quarters[m0 % BANK // QUARTER][:, c0 : c0 + width],
+                            ACT.Copy, scale=gain_sb[:, 1, t : t + 1],
+                        )
+        add_turned([standing[4 + last], sup_pages[last_pages]], pairs[1])
+        partial = pairs[0]
+        for half in range(T2 // BANK):
+            turn_back(pairs[1][half], ACT.Copy, [partial[half][:, b * P : (b + 1) * P] for b in range(4)])
 
         out_rows = out.rearrange("(j p) m -> p j m", p=P)
-        n_banks = N // P // N_PER_BANK
-        for m0 in range(0, T2, CHUNK):
-            z_on_vector(1, m0)
-            for bank in range(n_banks):
-                acc = psum.tile([P, N_PER_BANK, CHUNK], F32, name="acc", tag="acc", bufs=3)
-                for a in range(R_PASSES):
-                    for jj in range(N_PER_BANK):
-                        n0 = (bank * N_PER_BANK + jj) * P
-                        nc.tensor.matmul_mx(
-                            out=acc[:, jj, :],
-                            lhsT=wdis_sb[:, a, n0 : n0 + P].bitcast(FP8X4),
-                            lhsT_scale=wdis_plane[:, a * N + n0 : a * N + n0 + P],
-                            rhs=z_codes[a, m0].bitcast(FP8X4),
-                            rhs_scale=z_planes[a, m0],
-                            start=(a == 0 and jj == 0),
-                            stop=(a == R_PASSES - 1 and jj == N_PER_BANK - 1),
-                        )
-                result = ring.tile([P, N_PER_BANK, CHUNK], F32, name="result", tag="scores", bufs=12)
-                if m0 == T2 - CHUNK and bank != 1:
-                    nc.vector.tensor_copy(result[:], acc[:])
-                else:
-                    nc.scalar.copy(result[:], acc[:])
-                nc.sync.dma_start(
-                    out_rows[:, bank * N_PER_BANK : (bank + 1) * N_PER_BANK, m0 : m0 + CHUNK], result[:]
+        bank_order = [0, 1, 2, 7, 5, 6, 3, 4, 0, 1, 2, 7, 5]
+        groups = []
+        for m0, width in CHUNKS:
+            for j0 in range(0, N // P, BANK // width):
+                groups.append((m0, width, j0, min(BANK // width, N // P - j0), banks[bank_order[len(groups)]]))
+
+        def dispatch_pass(a, m0, width, j0, count, acc):
+            for jj in range(count):
+                n0 = (j0 + jj) * P
+                nc.tensor.matmul_mx(
+                    out=acc[:, jj * width : (jj + 1) * width],
+                    lhsT=wdis_sb[:, a, n0 : n0 + P].bitcast(FP8X4),
+                    lhsT_scale=wdis_plane[:, a * N + n0 : a * N + n0 + P],
+                    rhs=z_codes[a, m0].bitcast(FP8X4),
+                    rhs_scale=z_planes[a, m0],
+                    start=(a == 0 and jj == 0),
+                    stop=(a == R_PASSES - 1 and jj == count - 1),
                 )
+
+        for group in groups[:EARLY_GROUPS]:
+            dispatch_pass(0, *group)
+        last_page = dem_pages[last_pages]
+        place(last_page, dem_list, h2_planes[last], wg2_last)
+        for m0, width in CHUNKS:
+            half, c0 = divmod(m0, BANK)
+            total = ring.tile([P, width], F32, name="total", tag="total", bufs=5)
+            nc.vector.tensor_tensor(total[:], partial[half][:, c0 : c0 + width], last_page[:, m0 : m0 + width], ADD)
+            squashed = ring.tile([P, width], F32, name="squashed", tag="squashed", bufs=2)
+            nc.scalar.activation(squashed[:], total[:], ACT.Tanh)
+            nc.scalar.activation(z_rows[m0][:, last, :], squashed[:], ACT.Copy, scale=gain_sb[:, 1, last : last + 1])
+        for m0, width in CHUNKS:
+            woven = ring.tile([P, width, PACK], BF16, name="woven", tag="woven", bufs=4, align_bytes=64)
+            nc.vector.tensor_copy(
+                woven[:].rearrange("p (c i) t -> p c t i", i=4),
+                z_rows[m0][:].rearrange("p t (c i) -> p c t i", i=4),
+            )
+            quantize_z(1, m0, width, woven)
+        for g, group in enumerate(groups):
+            m0, width, j0, count, acc = group
+            if g >= EARLY_GROUPS:
+                dispatch_pass(0, *group)
+            dispatch_pass(1, *group)
+            result = ring.tile([P, count, width], F32, name="result", tag="scores", bufs=10)
+            source = acc[:, : count * width].rearrange("p (j m) -> p j m", j=count)
+            if g in (6, 8, 10, 12):
+                nc.vector.tensor_copy(result[:], source)
+            else:
+                nc.scalar.copy(result[:], source)
+            nc.sync.dma_start(out_rows[:, j0 : j0 + count, m0 : m0 + width], result[:])

@@ -23,17 +23,22 @@ PACK = 4
 K_PASS = P * PACK
 K_PASSES = K // K_PASS
 R_PASSES = H // K_PASS
-R_TILES = H // P
 BANK = 512
-M_BLOCKS = T2 // P
 BLOCKS_PER_BANK = BANK // P
-EARLY_TILES = 1
+HALVES = T2 // BANK
 PAGES = 3
-TAB_BYTES = 4 * T
-PAGE_BYTES = 4 * T2
 QUARTER = 256
+EARLY_COLS = 4 * P
+LIVE_ROWS = 100
+KIB = 1024
+CHUNKS = ((0, 128), (128, 128), (256, 256), (512, 512))
 EARLY_GROUPS = 6
-CHUNKS = ((0, 128), (128, 128), (256, 256), (512, 256), (768, 256))
+
+TAB_AT = 0
+LOTS_AT = 27 * KIB
+WOVEN_AT = 31 * KIB
+RAW_AT = 37 * KIB
+RAW_LATE_AT = 61 * KIB
 
 
 def tile_list_surplus_exchange_slots_kernel(
@@ -47,17 +52,21 @@ def tile_list_surplus_exchange_slots_kernel(
         shared = ctx.enter_context(tc.tile_pool(name="shared", bufs=1))
         psum = ctx.enter_context(tc.psum_pool(name="psum", bufs=1))
 
+        def placed(shape, dtype, name, offset):
+            return shared.tile(shape, dtype, name=name, offset=offset, align_bytes=64)
+
+        def kept(shape, dtype, name):
+            return keep.tile(shape, dtype, name=name, align_bytes=64)
+
         def load_list(source, name):
             tile = keep.tile([P, S // 16], U16, name=name)
             nc.sync.dma_start(tile[:], source)
             return tile
 
-        def zeroed_plane(width, name, engine):
-            plane = keep.tile([P, width], U8, name=name, align_bytes=64)
-            engine.memset(plane[:].bitcast(I32), 0)
-            return plane
+        def zero(tile, engine):
+            engine.memset(tile[:].bitcast(I32), 0)
 
-        def load_scale_rows(plane, source, cols, queue=nc.sync):
+        def load_scale_rows(plane, source, cols, queue):
             passes = source.shape[0]
             for quad in range(4):
                 queue.dma_start(
@@ -65,71 +74,77 @@ def tile_list_surplus_exchange_slots_kernel(
                     source[:, 4 * quad : 4 * quad + 4, cols].rearrange("a r c -> r a c").bitcast(I32),
                 )
 
-        def big_tile(shape, dtype, name):
-            return ring.tile(shape, dtype, name=name, tag="big", bufs=5, align_bytes=64)
-
-        early_cols = EARLY_TILES * P
-        late_cols = H - early_cols
-        tab_plane = zeroed_plane(K_PASSES * T, "tab_plane", nc.gpsimd)
-        wsup_plane_late = zeroed_plane(K_PASSES * late_cols, "wsup_plane_late", nc.vector)
-        wdis_plane = zeroed_plane(R_PASSES * N, "wdis_plane", nc.vector)
+        tab_plane = placed([P, T], U8, "tab_plane", LOTS_AT + KIB)
+        zero(tab_plane, nc.gpsimd)
+        wsup_plane_early = placed([P, K_PASSES * EARLY_COLS], U8, "wsup_plane_early", WOVEN_AT + 4 * KIB)
+        zero(wsup_plane_early, nc.gpsimd)
+        lot_planes = [kept([P, S], U8, f"lot_plane{a}") for a in range(K_PASSES)]
+        for a in range(1, K_PASSES):
+            zero(lot_planes[a], nc.vector)
         sup_pages = [keep.tile([P, T2], F32, name=f"sup_page{i}") for i in range(PAGES)]
         for page in sup_pages:
-            nc.vector.memset(page[:].bitcast(I32), 0)
-        wsup_plane_early = zeroed_plane(K_PASSES * early_cols, "wsup_plane_early", nc.vector)
+            zero(page, nc.vector)
 
         tab_tiles = []
 
         def load_tab(a):
-            tile = shared.tile([P, T], U32, name=f"tab{a}", offset=a * TAB_BYTES, align_bytes=64)
+            tile = placed([P, T], U32, f"tab{a}", TAB_AT + a * 4 * T)
             nc.sync.dma_start(tile[:].bitcast(I32), tab_words[a].rearrange("p t i -> p (t i)").bitcast(I32))
             tab_tiles.append(tile)
 
-        def load_wsup(c0, c1, name, queue):
-            tile = keep.tile([P, K_PASSES, 2 * (c1 - c0)], U8, name=name, align_bytes=64)
-            queue.dma_start(
+        def load_wsup(tile, c0, c1):
+            nc.sync.dma_start(
                 tile[:].bitcast(I32), wsup_words.rearrange("a p c -> p a c")[:, :, 2 * c0 : 2 * c1].bitcast(I32)
             )
             return tile
 
         load_tab(0)
+        for quad in range(4):
+            nc.scalar.dma_start(
+                tab_plane[32 * quad : 32 * quad + 4 * K_PASSES, :].bitcast(I32),
+                tab_scales[:, 4 * quad : 4 * quad + 4, :].bitcast(I32),
+            )
+        load_scale_rows(wsup_plane_early, wsup_scales, slice(0, EARLY_COLS), nc.gpsimd)
         lot_list = load_list(offs, "lot_list")
-        sup_list = load_list(offs2, "sup_list")
-        load_scale_rows(tab_plane, tab_scales, slice(0, T))
         load_tab(1)
+        wsup_first = load_wsup(placed([P, K_PASSES, 2 * P], U8, "wsup_first", WOVEN_AT + 2 * KIB - 384), 0, P)
         load_tab(2)
-        load_scale_rows(wsup_plane_early, wsup_scales, slice(0, early_cols), nc.scalar)
-        wsup_early = load_wsup(0, early_cols, "wsup_early", nc.scalar)
+        sup_list = load_list(offs2, "sup_list")
         wg1_sb = keep.tile([P, S], F32, name="wg1_sb")
         nc.sync.dma_start(wg1_sb[:], wg1)
-        load_scale_rows(wsup_plane_late, wsup_scales, slice(early_cols, H))
-        wsup_mid = load_wsup(early_cols, K_PASS, "wsup_mid", nc.sync)
+        wsup_mid = load_wsup(kept([P, K_PASSES, 2 * (K_PASS - P)], U8, "wsup_mid"), P, K_PASS)
 
-        lot_planes = []
-        lot_words = []
-        for a in range(K_PASSES):
-            plane = keep.tile([P, S], U8, name=f"lot_plane{a}", align_bytes=64)
-            nc.vector.tensor_copy(plane[:], tab_plane[:, a * T : (a + 1) * T].indirect(lot_list[:]))
-            lot_planes.append(plane)
-            words = keep.tile([P, S], U32, name=f"lot_words{a}", align_bytes=64)
-            nc.vector.tensor_copy(words[:], tab_tiles[a][:].indirect(lot_list[:]))
-            lot_words.append(words)
+        lot_words = [
+            kept([P, S], U32, "lot_words0"),
+            placed([P, S], U32, "lot_words1", LOTS_AT),
+            placed([P, S], U32, "lot_words2", LOTS_AT + 2 * KIB),
+        ]
+        nc.vector.tensor_copy(lot_words[0][:], tab_tiles[0][:].indirect(lot_list[:]))
+        nc.vector.tensor_copy(lot_planes[0][:], tab_plane[:].indirect(lot_list[:]))
+        for a in range(1, K_PASSES):
+            nc.scalar.dma_start(
+                lot_planes[a][:LIVE_ROWS, :].bitcast(I32), lot_planes[0][4 * a : 4 * a + LIVE_ROWS, :].bitcast(I32)
+            )
+        for a in range(1, K_PASSES):
+            nc.vector.tensor_copy(lot_words[a][:], tab_tiles[a][:].indirect(lot_list[:]))
 
-        spot = 2 * TAB_BYTES - PAGE_BYTES // 2
+        late_cols = H - EARLY_COLS
+        wsup_plane_late = placed([P, K_PASSES * late_cols], U8, "wsup_plane_late", TAB_AT + 8 * KIB)
+        zero(wsup_plane_late, nc.gpsimd)
         dem_pages = []
 
         def zeroed_page(name, offset):
-            page = shared.tile([P, T2], F32, name=name, offset=offset)
+            page = placed([P, T2], F32, name, offset)
             nc.gpsimd.memset(page[:], 0.0)
             dem_pages.append(page)
 
-        zeroed_page("dem_page0", spot)
-        zeroed_page("dem_page1", spot + PAGE_BYTES)
-        spot = spot + 2 * PAGE_BYTES
-        ident = shared.tile([P, P], F32, name="ident", offset=spot)
+        zeroed_page("dem_page0", TAB_AT + 14 * KIB)
+        zeroed_page("dem_page1", TAB_AT + 18 * KIB)
+        ident = placed([P, P], F32, "ident", TAB_AT + 22 * KIB)
         make_identity(nc, ident[:])
-        zeroed_page("dem_page2", spot + 4 * P)
-
+        zeroed_page("dem_page2", TAB_AT + 22 * KIB + 4 * P)
+        wdis_plane = placed([P, R_PASSES * N], U8, "wdis_plane", TAB_AT + 12 * KIB)
+        zero(wdis_plane, nc.gpsimd)
 
         banks = [psum.tile([P, BANK], F32, name=f"bank{i}") for i in range(8)]
         pairs = (banks[3:5], banks[5:7])
@@ -140,16 +155,20 @@ def tile_list_surplus_exchange_slots_kernel(
             return banks[(len(acc_turn) - 1) % 3]
 
         def score_tile():
-            return ring.tile([P, S], F32, name="scores", tag="scores", bufs=10)
+            return ring.tile([P, S], F32, name="scores", tag="scores", bufs=12)
 
-        def supply(i, words, plane, first_tile, width, h1):
-            c0 = (i - first_tile) * P
+        def supply(i, h1):
+            words, c0 = (wsup_first, 0) if i == 0 else (wsup_mid, (i - 1) * P)
+            if i * P < EARLY_COLS:
+                plane, width, s0 = wsup_plane_early, EARLY_COLS, i * P
+            else:
+                plane, width, s0 = wsup_plane_late, late_cols, i * P - EARLY_COLS
             acc = next_acc()
             for a in range(K_PASSES):
                 nc.tensor.matmul_mx(
                     out=acc[:],
                     lhsT=words[:, a, 2 * c0 : 2 * (c0 + P)].bitcast(FP4X4),
-                    lhsT_scale=plane[:, a * width + c0 : a * width + c0 + P],
+                    lhsT_scale=plane[:, a * width + s0 : a * width + s0 + P],
                     rhs=lot_words[a][:].bitcast(FP8X4),
                     rhs_scale=lot_planes[a][:],
                     start=(a == 0),
@@ -158,8 +177,9 @@ def tile_list_surplus_exchange_slots_kernel(
             nc.scalar.copy(h1, acc[:])
             return h1
 
-        def supply_turned(words, plane, c0, width):
-            turned = raws[3][:].rearrange("p j (t q) -> p j t q", t=PACK)
+        def supply_turned(words):
+            turned = placed([P, S // P, PACK, P], F32, "turned", TAB_AT)
+            s0 = K_PASS - EARLY_COLS
             for jb in range(S // P):
                 acc = next_acc()
                 for a in range(K_PASSES):
@@ -168,61 +188,57 @@ def tile_list_surplus_exchange_slots_kernel(
                         lhsT=lot_words[a][:, jb * P : (jb + 1) * P].bitcast(FP8X4),
                         lhsT_scale=lot_planes[a][:, jb * P : (jb + 1) * P],
                         rhs=words[:, a, :].bitcast(FP4X4),
-                        rhs_scale=plane[:, a * width + c0 : a * width + c0 + BANK],
+                        rhs_scale=wsup_plane_late[:, a * late_cols + s0 : a * late_cols + s0 + BANK],
                         start=(a == 0),
                         stop=(a == K_PASSES - 1),
                     )
                 nc.scalar.copy(turned[:, jb], acc[:].rearrange("j (p t) -> j t p", t=PACK))
             return turned
 
-        def supply_plane(turned, t):
+        def supply_plane(turned, t, h1):
             acc = next_acc()
             for jb in range(S // P):
                 nc.tensor.transpose(acc[:, jb * P : (jb + 1) * P], turned[:, jb, t, :], ident[:])
-            h1 = score_tile()
-            nc.scalar.copy(h1[:], acc[:])
-            return h1[:]
+            nc.scalar.copy(h1, acc[:])
+            return h1
 
         wdem_codes = {}
         wdem_planes = {}
-        raws = []
 
-        def quantize_wdem(half):
-            cols = slice(half * BANK, (half + 1) * BANK)
-            for a in range(K_PASSES):
-                raw = big_tile([P, PACK, BANK], F32, f"wdem_raw{half}{a}")
-                nc.sync.dma_start(
-                    raw[:], wdem[a * K_PASS : (a + 1) * K_PASS, cols].rearrange("(p j) c -> p j c", j=PACK)
-                )
-                woven = ring.tile([P, BANK, PACK], BF16, name="woven", tag="woven", bufs=4, align_bytes=64)
-                if half == 0:
-                    nc.scalar.copy(
-                        woven[:].rearrange("p (c i) j -> p c j i", i=4),
-                        raw[:].rearrange("p j (c i) -> p c j i", i=4),
-                    )
-                else:
-                    nc.scalar.copy(
-                        woven[:].rearrange("p (t q) j -> p q j t", t=PACK),
-                        raw[:].rearrange("p j (q t) -> p q j t", t=PACK),
-                    )
-                codes = keep.tile([P, BANK], U32, name=f"wdem_codes{half}{a}", align_bytes=64)
-                plane = keep.tile([P, BANK], U8, name=f"wdem_plane{half}{a}", align_bytes=64)
-                nc.vector.quantize_mx(
-                    out=codes[:].bitcast(FP8X4), scales=plane[:], in_=woven[:].rearrange("p c j -> p (c j)")
-                )
-                wdem_codes[half, a] = codes
-                wdem_planes[half, a] = plane
-                raws.append(raw)
+        def load_wdem(a, c0, width, offset):
+            raw = placed([P, PACK, width], F32, f"wdem_raw{a}_{c0}", offset)
+            nc.sync.dma_start(
+                raw[:], wdem[a * K_PASS : (a + 1) * K_PASS, c0 : c0 + width].rearrange("(p j) c -> p j c", j=PACK)
+            )
             return raw
 
-        def demand(i, h2):
-            half, c0 = divmod(i * P, BANK)
-            acc = next_acc()
+        def quantize_wdem(a, c0, raw, woven):
+            width = raw.shape[2]
+            if c0 < K_PASS:
+                nc.scalar.copy(
+                    woven[:].rearrange("p (c i) j -> p c j i", i=4),
+                    raw[:].rearrange("p j (c i) -> p c j i", i=4),
+                )
+            else:
+                nc.scalar.copy(
+                    woven[:].rearrange("p (t q) j -> p q j t", t=PACK),
+                    raw[:].rearrange("p j (q t) -> p q j t", t=PACK),
+                )
+            codes = kept([P, width], U32, f"wdem_codes{a}_{c0}")
+            plane = kept([P, width], U8, f"wdem_plane{a}_{c0}")
+            nc.vector.quantize_mx(
+                out=codes[:].bitcast(FP8X4), scales=plane[:], in_=woven[:].rearrange("p c j -> p (c j)")
+            )
+            for c in range(0, width, P):
+                wdem_codes[a, (c0 + c) // P] = codes[:, c : c + P]
+                wdem_planes[a, (c0 + c) // P] = plane[:, c : c + P]
+
+        def demand(i, h2, acc):
             for a in range(K_PASSES):
                 nc.tensor.matmul_mx(
                     out=acc[:],
-                    lhsT=wdem_codes[half, a][:, c0 : c0 + P].bitcast(FP8X4),
-                    lhsT_scale=wdem_planes[half, a][:, c0 : c0 + P],
+                    lhsT=wdem_codes[a, i].bitcast(FP8X4),
+                    lhsT_scale=wdem_planes[a, i],
                     rhs=lot_words[a][:].bitcast(FP8X4),
                     rhs_scale=lot_planes[a][:],
                     start=(a == 0),
@@ -234,14 +250,15 @@ def tile_list_surplus_exchange_slots_kernel(
         def place(page, slots, scores, weights):
             nc.vector.tensor_tensor(page[:].indirect(slots[:]), scores, weights, MULT)
 
-        def load_standing(rows):
-            standing = ring.tile([P, T2], F32, name="standing", tag="standing", bufs=4)
-            nc.sync.dma_start(standing[:], rows)
-            return standing
+        def load_standing(rows, tile=None):
+            if tile is None:
+                tile = ring.tile([P, T2], F32, name="standing", tag="standing", bufs=4)
+            nc.sync.dma_start(tile[:], rows)
+            return tile
 
         def add_turned(terms, total_banks):
             for n_term, term in enumerate(terms):
-                for half in range(T2 // BANK):
+                for half in range(HALVES):
                     for b in range(BLOCKS_PER_BANK):
                         m0 = half * BANK + b * P
                         nc.tensor.matmul(
@@ -257,17 +274,12 @@ def tile_list_surplus_exchange_slots_kernel(
             for b in range(BLOCKS_PER_BANK):
                 nc.tensor.transpose(targets[b], turned[:, b * P : (b + 1) * P], ident[:])
 
-        def load_dealt(target, source, t):
-            rows = source.rearrange("(q t) j -> q t j", t=PACK)[:, t, :]
-            for rep in range(P // 32):
-                nc.sync.dma_start(target[32 * rep : 32 * (rep + 1)], rows)
-
         z_codes = {}
         z_planes = {}
 
         def quantize_z(a, m0, width, woven):
-            codes = keep.tile([P, width], U32, name=f"z_codes{a}_{m0}", align_bytes=64)
-            plane = keep.tile([P, width], U8, name=f"z_plane{a}_{m0}", align_bytes=64)
+            codes = kept([P, width], U32, f"z_codes{a}_{m0}")
+            plane = kept([P, width], U8, f"z_plane{a}_{m0}")
             nc.vector.quantize_mx(
                 out=codes[:].bitcast(FP8X4), scales=plane[:], in_=woven[:].rearrange("p m t -> p (m t)")
             )
@@ -276,157 +288,186 @@ def tile_list_surplus_exchange_slots_kernel(
                     z_codes[a, c0] = codes[:, c0 - m0 : c0 - m0 + cw]
                     z_planes[a, c0] = plane[:, c0 - m0 : c0 - m0 + cw]
 
-        place(sup_pages[0], sup_list, supply(0, wsup_early, wsup_plane_early, 0, early_cols, score_tile()[:]), wg1_sb[:])
-        h1 = supply(1, wsup_mid, wsup_plane_late, EARLY_TILES, late_cols, score_tile()[:])
-        place(sup_pages[1], sup_list, h1, wg1_sb[:])
-        last_raw = quantize_wdem(0)
+        def words_of(pair_tile, dtype):
+            return pair_tile[:].rearrange("p u m e -> p (u m e)").bitcast(dtype).rearrange("p (u m) -> p m u", u=2)
+
+        def woven_words(woven, dtype):
+            return woven[:].rearrange("p m t -> p (m t)").bitcast(dtype).rearrange("p (m u) -> p m u", u=2)
+
+        place(sup_pages[0], sup_list, supply(0, score_tile()[:]), wg1_sb[:])
+        place(sup_pages[1], sup_list, supply(1, score_tile()[:]), wg1_sb[:])
+        raw_at = (4, 8, 0, 12, 16, 20)
+        raws = [load_wdem(a, 0, QUARTER, RAW_AT + raw_at[a] * KIB) for a in range(K_PASSES)]
+        for a in range(K_PASSES):
+            quantize_wdem(a, 0, raws[a], placed([P, QUARTER, PACK], BF16, f"woven{a}_0", WOVEN_AT + 2 * a * KIB))
+        h1_tile3 = supply(3, score_tile()[:])
+        h1 = supply(2, raws[2][:].rearrange("p j c -> p (j c)")[:, :S])
+        place(sup_pages[2], sup_list, h1, wg1_sb[:])
+        h2_tiles = [demand(i, score_tile()[:], next_acc()) for i in range(2)]
+        for a in range(K_PASSES):
+            raw = load_wdem(a, QUARTER, QUARTER, RAW_AT + raw_at[K_PASSES + a] * KIB)
+            quantize_wdem(a, QUARTER, raw, placed([P, QUARTER, PACK], BF16, f"woven{a}_1", WOVEN_AT + 2 * a * KIB))
+        late_raws = []
+
+        def quantize_late(a):
+            late_raws.append(load_wdem(a, K_PASS, K_PASS, RAW_LATE_AT + 8 * a * KIB))
+            woven = ring.tile([P, K_PASS, PACK], BF16, name="woven", tag="woven", bufs=3, align_bytes=64)
+            quantize_wdem(a, K_PASS, late_raws[a], woven)
+
+        quantize_late(0)
+        dem_list = load_list(offs3, "dem_list")
         wg2_sb = keep.tile([P, S], F32, name="wg2_sb")
         nc.sync.dma_start(wg2_sb[:], wg2)
-        dem_list = load_list(offs3, "dem_list")
-        h1 = supply(2, wsup_mid, wsup_plane_late, EARLY_TILES, late_cols, last_raw[:, 0, :])
-        place(sup_pages[2], sup_list, h1, wg1_sb[:])
-        quantize_wdem(1)
+        h2_tiles.append(demand(2, score_tile()[:], next_acc()))
         for i in range(PAGES):
-            place(dem_pages[i], dem_list, demand(i, raws[4][:, i, :]), wg2_sb[:])
-        h1_tile3 = supply(3, wsup_mid, wsup_plane_late, EARLY_TILES, late_cols, raws[5][:, 0, :])
-        h2_tile3 = demand(3, raws[5][:, 1, :])
-        wsup_late = load_wsup(K_PASS, H, "wsup_late", nc.sync)
-        standing = [load_standing(stand[0:P, :])]
-        sup_turned = supply_turned(wsup_late, wsup_plane_late, K_PASS - early_cols, late_cols)
-        h1_planes = [supply_plane(sup_turned, t) for t in range(PACK)]
-        standing.append(load_standing(stand[P : 2 * P, :]))
-        standing.append(load_standing(stand[2 * P : 3 * P, :]))
-        standing.append(load_standing(stand[3 * P : 4 * P, :]))
-        wg1_dealt = [keep.tile([P, S], F32, name=f"wg1_dealt{t}") for t in range(PACK)]
-        wg2_dealt = [keep.tile([P, S], F32, name=f"wg2_dealt{t}") for t in range(PACK - 1)]
-        for t in range(PACK):
-            load_dealt(wg1_dealt[t][:], wg1, t)
-            if t < PACK - 1:
-                load_dealt(wg2_dealt[t][:], wg2, t)
-        gain_sb = keep.tile([P, R_PASSES, PACK], F32, name="gain_sb")
-        nc.sync.dma_start(gain_sb[:], gain.rearrange("(a p t) -> p a t", p=P, t=PACK))
-        wdis_sb = keep.tile([P, R_PASSES, N], U32, name="wdis_sb", align_bytes=64)
-        nc.sync.dma_start(wdis_sb[:].bitcast(I32), wdis_words.rearrange("a p c i -> p a (c i)").bitcast(I32))
-        load_scale_rows(wdis_plane, wdis_scales, slice(0, N))
+            place(dem_pages[i], dem_list, h2_tiles[i], wg2_sb[:])
+        for a in range(1, K_PASSES):
+            quantize_late(a)
+        h2_tiles.append(demand(3, late_raws[2][:, 0, :], next_acc()))
+        standing = [load_standing(stand[i * P : (i + 1) * P, :]) for i in range(2)]
+        load_scale_rows(wsup_plane_late, wsup_scales, slice(EARLY_COLS, H), nc.sync)
+        wsup_late = load_wsup(kept([P, K_PASSES, 2 * K_PASS], U8, "wsup_late"), K_PASS, H)
+        sup_turned = supply_turned(wsup_late)
+        h1_planes = [supply_plane(sup_turned, t, score_tile()[:]) for t in range(PACK - 1)]
 
-        stand_planes = stand[K_PASS:, :].rearrange("(p t) m -> p t m", t=PACK)
-        bounded = [big_tile([P, BLOCKS_PER_BANK, PACK, P], F32, f"bounded{half}") for half in range(T2 // BANK)]
-        for i in range(4):
+        bounded = [
+            placed([P, BLOCKS_PER_BANK, PACK, P], F32, f"bounded{half}", RAW_AT + (16 - 8 * half) * KIB)
+            for half in range(HALVES)
+        ]
+
+        def bound_tile(i):
             total_banks = pairs[i % 2]
             add_turned([standing[i], sup_pages[i % PAGES], dem_pages[i % PAGES]], total_banks)
-            if i == 1:
-                h2_planes = [demand(4 + t, score_tile()[:]) for t in range(PACK)]
-            if i == 0:
-                place(sup_pages[0], sup_list, h1_tile3, wg1_sb[:])
-                place(dem_pages[0], dem_list, h2_tile3, wg2_sb[:])
-            else:
-                place(sup_pages[i % PAGES], sup_list, h1_planes[i - 1], wg1_dealt[i - 1][:])
-                place(dem_pages[i % PAGES], dem_list, h2_planes[i - 1], wg2_dealt[i - 1][:])
-            for half in range(T2 // BANK):
+            for half in range(HALVES):
                 nc.scalar.activation(
                     bounded[half][:, :, :, 32 * i : 32 * (i + 1)],
                     total_banks[half][:].rearrange("m (b q t) -> m b t q", b=BLOCKS_PER_BANK, t=PACK),
                     ACT.Tanh,
                 )
-            standing.append(load_standing(stand_planes[:, i, :]))
 
-        z0_banks = [7, 0, 1, 2, 7, 0, 5, 6]
-        z0_rows = []
-        for half in range(T2 // BANK):
-            rows = ring.tile([P, PACK, BANK], BF16, name="z_rows", tag="woven", bufs=4, align_bytes=64)
-            z0_rows.append(rows)
+        bound_tile(0)
+        place(sup_pages[0], sup_list, h1_tile3, wg1_sb[:])
+        place(dem_pages[0], dem_list, h2_tiles[3], wg2_sb[:])
+        bound_tile(1)
+        wg1_dealt = keep.tile([P, PACK, S], F32, name="wg1_dealt")
+        wg2_dealt = keep.tile([P, PACK, S], F32, name="wg2_dealt")
+        for rep in range(P // 32):
+            for dealt, source in ((wg1_dealt, wg1), (wg2_dealt, wg2)):
+                nc.sync.dma_start(dealt[32 * rep : 32 * (rep + 1)], source.rearrange("(q t) j -> q t j", t=PACK))
+        standing.append(load_standing(stand[2 * P : 3 * P, :]))
+        standing.append(load_standing(stand[3 * P : 4 * P, :]))
+        gain_sb = keep.tile([P, R_PASSES, PACK], F32, name="gain_sb")
+        nc.sync.dma_start(gain_sb[:], gain.rearrange("(a p t) -> p a t", p=P, t=PACK))
+        stand_planes = stand[K_PASS:, :].rearrange("(p t) m -> p t m", t=PACK)
+        standing.append(load_standing(stand_planes[:, 0, :]))
+        standing.append(load_standing(stand_planes[:, 1, :]))
+        wdis_sb = kept([P, R_PASSES, N], U32, "wdis_sb")
+        nc.sync.dma_start(wdis_sb[:].bitcast(I32), wdis_words.rearrange("a p c i -> p a (c i)").bitcast(I32))
+        load_scale_rows(wdis_plane, wdis_scales, slice(0, N), nc.sync)
+
+        plane_accs = (pairs[1][0], pairs[1][1], next_acc())
+        h2_planes = [demand(PACK + t, score_tile()[:], plane_accs[t]) for t in range(PACK - 1)]
+        bound_tile(2)
+        place(sup_pages[1], sup_list, h1_planes[0], wg1_dealt[:, 0, :])
+        place(dem_pages[1], dem_list, h2_planes[0], wg2_dealt[:, 0, :])
+        bound_tile(3)
+        for t in range(1, PACK - 1):
+            place(sup_pages[(4 + t) % PAGES], sup_list, h1_planes[t], wg1_dealt[:, t, :])
+            place(dem_pages[(4 + t) % PAGES], dem_list, h2_planes[t], wg2_dealt[:, t, :])
+
+        z0_banks = (7, 0, 1, 2, 7, 0, 5, 6)
+        for half in range(HALVES):
+            rows = placed([P, 2, BANK, 2], BF16, f"z0_pairs{half}", RAW_LATE_AT + 4 * half * KIB)
             for t in range(PACK):
                 back = banks[z0_banks[half * PACK + t]]
                 for b in range(BLOCKS_PER_BANK):
                     nc.tensor.transpose(back[:, b * P : (b + 1) * P], bounded[half][:, b, t, :], ident[:])
-                nc.scalar.activation(rows[:, t, :], back[:], ACT.Copy, scale=gain_sb[:, 0, t : t + 1])
-        for half in range(T2 // BANK):
-            rows = z0_rows[half]
-            woven = ring.tile([P, BANK, PACK], BF16, name="woven", tag="woven", bufs=4, align_bytes=64)
-            nc.scalar.copy(
-                woven[:].rearrange("p (c i) t -> p c t i", i=4),
-                rows[:].rearrange("p t (c i) -> p c t i", i=4),
-            )
+                nc.scalar.activation(rows[:, t // 2, :, t % 2], back[:], ACT.Copy, scale=gain_sb[:, 0, t : t + 1])
+            woven = placed([P, BANK, PACK], BF16, f"z0_woven{half}", RAW_LATE_AT + (8 + 4 * half) * KIB)
+            nc.scalar.copy(woven_words(woven, U32), words_of(rows, U32))
             quantize_z(0, half * BANK, BANK, woven)
-        wg2_last = z0_rows[1][:].rearrange("p t m -> p (t m)").bitcast(F32)[:, :S]
-        load_dealt(wg2_last, wg2, PACK - 1)
-
-        z_rows = {m0: keep.tile([P, PACK, width], BF16, name=f"z_rows{m0}") for m0, width in CHUNKS}
         last = PACK - 1
+        h1_last = placed([P, S], F32, "h1_last", RAW_LATE_AT + 4 * KIB)
+        h1_planes.append(supply_plane(sup_turned, last, h1_last[:]))
+        h2_last = placed([P, S], F32, "h2_last", RAW_LATE_AT + 6 * KIB)
+        h2_planes.append(demand(PACK + last, h2_last[:], next_acc()))
+        for t in range(2, PACK):
+            standing.append(load_standing(stand_planes[:, t, :], placed([P, T2], F32, f"standing{t}", RAW_AT + 4 * t * KIB)))
+
+        z_pairs = {
+            m0: placed([P, 2, width, 2], BF16, f"z1_pairs{m0}", RAW_LATE_AT + 16 * KIB + 8 * m0) for m0, width in CHUNKS
+        }
         last_pages = (4 + last) % PAGES
         for t in range(last):
             total_banks = pairs[t % 2]
             add_turned([standing[4 + t], sup_pages[(4 + t) % PAGES], dem_pages[(4 + t) % PAGES]], total_banks)
             if t == 0:
-                place(sup_pages[last_pages], sup_list, h1_planes[last], wg1_dealt[last][:])
-            for half in range(T2 // BANK):
-                if t < last - 1:
-                    back = banks[((1, 2), (7, 0))[t][half]]
-                    quarters = [back[:, :QUARTER], back[:, QUARTER:]]
-                else:
-                    quarters = [banks[b][:, :QUARTER] for b in ((0, 1), (2, 7))[half]]
-                turn_back(
-                    total_banks[half], ACT.Tanh, [quarters[b // 2][:, b % 2 * P : (b % 2 + 1) * P] for b in range(4)]
-                )
+                place(sup_pages[last_pages], sup_list, h1_planes[last], wg1_dealt[:, last, :])
+            for half in range(HALVES):
+                back = banks[((1, 2), (7, 0), (1, 2))[t][half]]
+                turn_back(total_banks[half], ACT.Tanh, [back[:, b * P : (b + 1) * P] for b in range(4)])
                 for m0, width in CHUNKS:
                     if m0 // BANK == half:
-                        c0 = m0 % QUARTER
+                        c0 = m0 % BANK
                         nc.scalar.activation(
-                            z_rows[m0][:, t, :], quarters[m0 % BANK // QUARTER][:, c0 : c0 + width],
+                            z_pairs[m0][:, t // 2, :, t % 2], back[:, c0 : c0 + width],
                             ACT.Copy, scale=gain_sb[:, 1, t : t + 1],
                         )
         add_turned([standing[4 + last], sup_pages[last_pages]], pairs[1])
         partial = pairs[0]
-        for half in range(T2 // BANK):
+        for half in range(HALVES):
             turn_back(pairs[1][half], ACT.Copy, [partial[half][:, b * P : (b + 1) * P] for b in range(4)])
 
         out_rows = out.rearrange("(j p) m -> p j m", p=P)
-        bank_order = [0, 1, 2, 7, 5, 6, 3, 4, 0, 1, 2, 7, 5]
-        groups = []
-        for m0, width in CHUNKS:
-            for j0 in range(0, N // P, BANK // width):
-                groups.append((m0, width, j0, min(BANK // width, N // P - j0), banks[bank_order[len(groups)]]))
+        bank_order = (7, 0, 1, 2, 5, 6, 3, 4, 7, 0, 1, 2)
+        parts = [
+            [(0, j) for j in range(4)], [(128, j) for j in range(4)], [(0, 4), (128, 4), (0, 5), (128, 5)],
+        ]
+        parts = parts + [[(256, j), (256, j + 1)] for j in range(0, 6, 2)] + [[(512, j)] for j in range(6)]
+        widths = dict(CHUNKS)
 
-        def dispatch_pass(a, m0, width, j0, count, acc):
-            for jj in range(count):
-                n0 = (j0 + jj) * P
+        def dispatch_pass(a, g):
+            acc = banks[bank_order[g]]
+            for n_part, (m0, j) in enumerate(parts[g]):
+                width = widths[m0]
                 nc.tensor.matmul_mx(
-                    out=acc[:, jj * width : (jj + 1) * width],
-                    lhsT=wdis_sb[:, a, n0 : n0 + P].bitcast(FP8X4),
-                    lhsT_scale=wdis_plane[:, a * N + n0 : a * N + n0 + P],
+                    out=acc[:, n_part * width : (n_part + 1) * width],
+                    lhsT=wdis_sb[:, a, j * P : (j + 1) * P].bitcast(FP8X4),
+                    lhsT_scale=wdis_plane[:, a * N + j * P : a * N + (j + 1) * P],
                     rhs=z_codes[a, m0].bitcast(FP8X4),
                     rhs_scale=z_planes[a, m0],
-                    start=(a == 0 and jj == 0),
-                    stop=(a == R_PASSES - 1 and jj == count - 1),
+                    start=(a == 0 and n_part == 0),
+                    stop=(a == R_PASSES - 1 and n_part == len(parts[g]) - 1),
                 )
 
-        for group in groups[:EARLY_GROUPS]:
-            dispatch_pass(0, *group)
+        for g in range(EARLY_GROUPS):
+            dispatch_pass(0, g)
         last_page = dem_pages[last_pages]
-        place(last_page, dem_list, h2_planes[last], wg2_last)
+        place(last_page, dem_list, h2_planes[last], wg2_dealt[:, last, :])
         for m0, width in CHUNKS:
             half, c0 = divmod(m0, BANK)
-            total = ring.tile([P, width], F32, name="total", tag="total", bufs=5)
+            total = kept([P, width], F32, f"total{m0}")
             nc.vector.tensor_tensor(total[:], partial[half][:, c0 : c0 + width], last_page[:, m0 : m0 + width], ADD)
-            squashed = ring.tile([P, width], F32, name="squashed", tag="squashed", bufs=2)
+            squashed = kept([P, width], F32, f"squashed{m0}")
             nc.scalar.activation(squashed[:], total[:], ACT.Tanh)
-            nc.scalar.activation(z_rows[m0][:, last, :], squashed[:], ACT.Copy, scale=gain_sb[:, 1, last : last + 1])
-        for m0, width in CHUNKS:
-            woven = ring.tile([P, width, PACK], BF16, name="woven", tag="woven", bufs=4, align_bytes=64)
-            nc.vector.tensor_copy(
-                woven[:].rearrange("p (c i) t -> p c t i", i=4),
-                z_rows[m0][:].rearrange("p t (c i) -> p c t i", i=4),
+            nc.scalar.activation(
+                z_pairs[m0][:, 1, :, 1], squashed[:], ACT.Copy, scale=gain_sb[:, 1, last : last + 1]
             )
+        for m0, width in CHUNKS:
+            woven = placed([P, width, PACK], BF16, f"z1_woven{m0}", TAB_AT + 8 * m0)
+            nc.vector.tensor_copy(woven_words(woven, I32), words_of(z_pairs[m0], I32))
             quantize_z(1, m0, width, woven)
-        for g, group in enumerate(groups):
-            m0, width, j0, count, acc = group
+        for g in range(len(parts)):
             if g >= EARLY_GROUPS:
-                dispatch_pass(0, *group)
-            dispatch_pass(1, *group)
-            result = ring.tile([P, count, width], F32, name="result", tag="scores", bufs=10)
-            source = acc[:, : count * width].rearrange("p (j m) -> p j m", j=count)
-            if g in (6, 8, 10, 12):
-                nc.vector.tensor_copy(result[:], source)
+                dispatch_pass(0, g)
+            dispatch_pass(1, g)
+            result = score_tile()
+            if g in (6, 8, 10):
+                nc.vector.tensor_copy(result[:], banks[bank_order[g]][:])
             else:
-                nc.scalar.copy(result[:], source)
-            nc.sync.dma_start(out_rows[:, j0 : j0 + count, m0 : m0 + width], result[:])
+                nc.scalar.copy(result[:], banks[bank_order[g]][:])
+            m0, j0 = parts[g][0]
+            tiles = parts[g][-1][1] - j0 + 1
+            nc.sync.dma_start(
+                out_rows[:, j0 : j0 + tiles, m0 : m0 + BANK // tiles], result[:].rearrange("p (j m) -> p j m", j=tiles)
+            )

@@ -104,7 +104,7 @@ def tile_list_surplus_exchange_slots_kernel(
                 tab_plane[32 * quad : 32 * quad + 4 * K_PASSES, :].bitcast(I32),
                 tab_scales[:, 4 * quad : 4 * quad + 4, :].bitcast(I32),
             )
-        load_scale_rows(wsup_plane_early, wsup_scales, slice(0, EARLY_COLS), nc.gpsimd)
+        load_scale_rows(wsup_plane_early, wsup_scales, slice(0, EARLY_COLS), nc.scalar)
         lot_list = load_list(offs, "lot_list")
         load_tab(1)
         wsup_first = load_wsup(placed([P, K_PASSES, 2 * P], U8, "wsup_first", WOVEN_AT + 2 * KIB - 384), 0, P)

@@ -26,8 +26,9 @@ R_PASSES = H // K_PASS
 BANK = 512
 BLOCKS_PER_BANK = BANK // P
 HALVES = T2 // BANK
-PAGES = 3
 QUARTER = 256
+SUP_PAGES = 3
+DEM_PAGES = 3
 EARLY_COLS = 4 * P
 LIVE_ROWS = 100
 KIB = 1024
@@ -75,13 +76,13 @@ def tile_list_surplus_exchange_slots_kernel(
                 )
 
         tab_plane = placed([P, T], U8, "tab_plane", LOTS_AT + KIB)
-        zero(tab_plane, nc.gpsimd)
+        zero(tab_plane, nc.vector)
         wsup_plane_early = placed([P, K_PASSES * EARLY_COLS], U8, "wsup_plane_early", WOVEN_AT + 4 * KIB)
         zero(wsup_plane_early, nc.gpsimd)
         lot_planes = [kept([P, S], U8, f"lot_plane{a}") for a in range(K_PASSES)]
         for a in range(1, K_PASSES):
             zero(lot_planes[a], nc.vector)
-        sup_pages = [keep.tile([P, T2], F32, name=f"sup_page{i}") for i in range(PAGES)]
+        sup_pages = [keep.tile([P, T2], F32, name=f"sup_page{i}") for i in range(SUP_PAGES)]
         for page in sup_pages:
             zero(page, nc.vector)
 
@@ -108,8 +109,8 @@ def tile_list_surplus_exchange_slots_kernel(
         lot_list = load_list(offs, "lot_list")
         load_tab(1)
         wsup_first = load_wsup(placed([P, K_PASSES, 2 * P], U8, "wsup_first", WOVEN_AT + 2 * KIB - 384), 0, P)
-        load_tab(2)
         sup_list = load_list(offs2, "sup_list")
+        load_tab(2)
         wg1_sb = keep.tile([P, S], F32, name="wg1_sb")
         nc.sync.dma_start(wg1_sb[:], wg1)
         wsup_mid = load_wsup(kept([P, K_PASSES, 2 * (K_PASS - P)], U8, "wsup_mid"), P, K_PASS)
@@ -157,13 +158,12 @@ def tile_list_surplus_exchange_slots_kernel(
         def score_tile():
             return ring.tile([P, S], F32, name="scores", tag="scores", bufs=12)
 
-        def supply(i, h1):
+        def supply(i, h1, acc):
             words, c0 = (wsup_first, 0) if i == 0 else (wsup_mid, (i - 1) * P)
             if i * P < EARLY_COLS:
                 plane, width, s0 = wsup_plane_early, EARLY_COLS, i * P
             else:
                 plane, width, s0 = wsup_plane_late, late_cols, i * P - EARLY_COLS
-            acc = next_acc()
             for a in range(K_PASSES):
                 nc.tensor.matmul_mx(
                     out=acc[:],
@@ -294,50 +294,17 @@ def tile_list_surplus_exchange_slots_kernel(
         def woven_words(woven, dtype):
             return woven[:].rearrange("p m t -> p (m t)").bitcast(dtype).rearrange("p (m u) -> p m u", u=2)
 
-        place(sup_pages[0], sup_list, supply(0, score_tile()[:]), wg1_sb[:])
-        place(sup_pages[1], sup_list, supply(1, score_tile()[:]), wg1_sb[:])
-        raw_at = (4, 8, 0, 12, 16, 20)
-        raws = [load_wdem(a, 0, QUARTER, RAW_AT + raw_at[a] * KIB) for a in range(K_PASSES)]
-        for a in range(K_PASSES):
-            quantize_wdem(a, 0, raws[a], placed([P, QUARTER, PACK], BF16, f"woven{a}_0", WOVEN_AT + 2 * a * KIB))
-        h1_tile3 = supply(3, score_tile()[:])
-        h1 = supply(2, raws[2][:].rearrange("p j c -> p (j c)")[:, :S])
-        place(sup_pages[2], sup_list, h1, wg1_sb[:])
-        h2_tiles = [demand(i, score_tile()[:], next_acc()) for i in range(2)]
-        for a in range(K_PASSES):
-            raw = load_wdem(a, QUARTER, QUARTER, RAW_AT + raw_at[K_PASSES + a] * KIB)
-            quantize_wdem(a, QUARTER, raw, placed([P, QUARTER, PACK], BF16, f"woven{a}_1", WOVEN_AT + 2 * a * KIB))
-        late_raws = []
-
-        def quantize_late(a):
-            late_raws.append(load_wdem(a, K_PASS, K_PASS, RAW_LATE_AT + 8 * a * KIB))
-            woven = ring.tile([P, K_PASS, PACK], BF16, name="woven", tag="woven", bufs=3, align_bytes=64)
-            quantize_wdem(a, K_PASS, late_raws[a], woven)
-
-        quantize_late(0)
-        dem_list = load_list(offs3, "dem_list")
-        wg2_sb = keep.tile([P, S], F32, name="wg2_sb")
-        nc.sync.dma_start(wg2_sb[:], wg2)
-        h2_tiles.append(demand(2, score_tile()[:], next_acc()))
-        for i in range(PAGES):
-            place(dem_pages[i], dem_list, h2_tiles[i], wg2_sb[:])
-        for a in range(1, K_PASSES):
-            quantize_late(a)
-        h2_tiles.append(demand(3, late_raws[2][:, 0, :], next_acc()))
-        standing = [load_standing(stand[i * P : (i + 1) * P, :]) for i in range(2)]
-        load_scale_rows(wsup_plane_late, wsup_scales, slice(EARLY_COLS, H), nc.sync)
-        wsup_late = load_wsup(kept([P, K_PASSES, 2 * K_PASS], U8, "wsup_late"), K_PASS, H)
-        sup_turned = supply_turned(wsup_late)
-        h1_planes = [supply_plane(sup_turned, t, score_tile()[:]) for t in range(PACK - 1)]
-
         bounded = [
             placed([P, BLOCKS_PER_BANK, PACK, P], F32, f"bounded{half}", RAW_AT + (16 - 8 * half) * KIB)
             for half in range(HALVES)
         ]
 
+        def pages_of(i):
+            return [sup_pages[i % SUP_PAGES], dem_pages[i % DEM_PAGES]]
+
         def bound_tile(i):
             total_banks = pairs[i % 2]
-            add_turned([standing[i], sup_pages[i % PAGES], dem_pages[i % PAGES]], total_banks)
+            add_turned([standing[i]] + pages_of(i), total_banks)
             for half in range(HALVES):
                 nc.scalar.activation(
                     bounded[half][:, :, :, 32 * i : 32 * (i + 1)],
@@ -345,35 +312,83 @@ def tile_list_surplus_exchange_slots_kernel(
                     ACT.Tanh,
                 )
 
+        for i in range(2):
+            place(sup_pages[i], sup_list, supply(i, score_tile()[:], next_acc()), wg1_sb[:])
+
+        def quantize_quarter(quarter, raw_at):
+            raws = [load_wdem(a, quarter * QUARTER, QUARTER, RAW_AT + raw_at[a] * KIB) for a in range(K_PASSES)]
+            for a in range(K_PASSES):
+                woven = placed([P, QUARTER, PACK], BF16, f"woven{a}_{quarter}", WOVEN_AT + 2 * a * KIB)
+                quantize_wdem(a, quarter * QUARTER, raws[a], woven)
+            return raws[-1][:].rearrange("p j c -> p (j c)")[:, :S]
+
+        late_raws = []
+
+        def quantize_late(a):
+            late_raws.append(load_wdem(a, K_PASS, K_PASS, RAW_LATE_AT + 8 * a * KIB))
+            woven = ring.tile([P, K_PASS, PACK], BF16, name="woven", tag="woven", bufs=3, align_bytes=64)
+            quantize_wdem(a, K_PASS, late_raws[a], woven)
+
+        place(sup_pages[2], sup_list, supply(2, quantize_quarter(0, (8, 12, 0)), next_acc()), wg1_sb[:])
+        dem_list = load_list(offs3, "dem_list")
+        wg2_sb = keep.tile([P, S], F32, name="wg2_sb")
+        nc.sync.dma_start(wg2_sb[:], wg2)
+        standing = [load_standing(stand[0:P, :])]
+        for i in range(2):
+            place(dem_pages[i], dem_list, demand(i, score_tile()[:], next_acc()), wg2_sb[:])
+        h1_tile3 = supply(3, quantize_quarter(1, (16, 20, 4)), banks[7])
+        load_scale_rows(wsup_plane_late, wsup_scales, slice(EARLY_COLS, H), nc.sync)
+        wsup_late = load_wsup(kept([P, K_PASSES, 2 * K_PASS], U8, "wsup_late"), K_PASS, H)
+        sup_turned = supply_turned(wsup_late)
         bound_tile(0)
         place(sup_pages[0], sup_list, h1_tile3, wg1_sb[:])
-        place(dem_pages[0], dem_list, h2_tiles[3], wg2_sb[:])
+        quantize_late(0)
+        place(dem_pages[2], dem_list, demand(2, late_raws[0][:, 0, :], next_acc()), wg2_sb[:])
+        h2_tile3 = demand(3, late_raws[0][:, 1, :], next_acc())
+        place(dem_pages[0], dem_list, h2_tile3, wg2_sb[:])
+        standing.append(load_standing(stand[P : 2 * P, :]))
         bound_tile(1)
-        wg1_dealt = keep.tile([P, PACK, S], F32, name="wg1_dealt")
-        wg2_dealt = keep.tile([P, PACK, S], F32, name="wg2_dealt")
-        for rep in range(P // 32):
-            for dealt, source in ((wg1_dealt, wg1), (wg2_dealt, wg2)):
-                nc.sync.dma_start(dealt[32 * rep : 32 * (rep + 1)], source.rearrange("(q t) j -> q t j", t=PACK))
+        for a in range(1, K_PASSES):
+            quantize_late(a)
         standing.append(load_standing(stand[2 * P : 3 * P, :]))
         standing.append(load_standing(stand[3 * P : 4 * P, :]))
+        h1_planes = [supply_plane(sup_turned, 0, late_raws[2][:, 1, :])]
+        h1_planes = h1_planes + [supply_plane(sup_turned, t, score_tile()[:]) for t in range(1, PACK - 1)]
+
+        wg1_dealt = []
+        wg2_dealt = []
+
+        def load_dealt(t):
+            for dealt, source, name in ((wg1_dealt, wg1, "wg1"), (wg2_dealt, wg2, "wg2")):
+                tile = keep.tile([P, S], F32, name=f"{name}_dealt{t}")
+                for rep in range(P // 32):
+                    nc.sync.dma_start(
+                        tile[32 * rep : 32 * (rep + 1)], source.rearrange("(q t) j -> q t j", t=PACK)[:, t, :]
+                    )
+                dealt.append(tile)
+
+        def place_plane(t):
+            sup_page, dem_page = pages_of(PACK + t)
+            place(sup_page, sup_list, h1_planes[t], wg1_dealt[t][:])
+            place(dem_page, dem_list, h2_planes[t], wg2_dealt[t][:])
+
+        bound_tile(2)
+        bound_tile(3)
+        h2_planes = [demand(PACK + t, score_tile()[:], next_acc()) for t in range(PACK - 1)]
+        for t in range(PACK - 1):
+            load_dealt(t)
         gain_sb = keep.tile([P, R_PASSES, PACK], F32, name="gain_sb")
         nc.sync.dma_start(gain_sb[:], gain.rearrange("(a p t) -> p a t", p=P, t=PACK))
         stand_planes = stand[K_PASS:, :].rearrange("(p t) m -> p t m", t=PACK)
         standing.append(load_standing(stand_planes[:, 0, :]))
         standing.append(load_standing(stand_planes[:, 1, :]))
+        load_dealt(3)
         wdis_sb = kept([P, R_PASSES, N], U32, "wdis_sb")
         nc.sync.dma_start(wdis_sb[:].bitcast(I32), wdis_words.rearrange("a p c i -> p a (c i)").bitcast(I32))
         load_scale_rows(wdis_plane, wdis_scales, slice(0, N), nc.sync)
 
-        plane_accs = (pairs[1][0], pairs[1][1], next_acc())
-        h2_planes = [demand(PACK + t, score_tile()[:], plane_accs[t]) for t in range(PACK - 1)]
-        bound_tile(2)
-        place(sup_pages[1], sup_list, h1_planes[0], wg1_dealt[:, 0, :])
-        place(dem_pages[1], dem_list, h2_planes[0], wg2_dealt[:, 0, :])
-        bound_tile(3)
-        for t in range(1, PACK - 1):
-            place(sup_pages[(4 + t) % PAGES], sup_list, h1_planes[t], wg1_dealt[:, t, :])
-            place(dem_pages[(4 + t) % PAGES], dem_list, h2_planes[t], wg2_dealt[:, t, :])
+        for t in range(PACK - 1):
+            place_plane(t)
 
         z0_banks = (7, 0, 1, 2, 7, 0, 5, 6)
         for half in range(HALVES):
@@ -397,12 +412,12 @@ def tile_list_surplus_exchange_slots_kernel(
         z_pairs = {
             m0: placed([P, 2, width, 2], BF16, f"z1_pairs{m0}", RAW_LATE_AT + 16 * KIB + 8 * m0) for m0, width in CHUNKS
         }
-        last_pages = (4 + last) % PAGES
+        last_sup, last_page = pages_of(PACK + last)
         for t in range(last):
             total_banks = pairs[t % 2]
-            add_turned([standing[4 + t], sup_pages[(4 + t) % PAGES], dem_pages[(4 + t) % PAGES]], total_banks)
+            add_turned([standing[PACK + t]] + pages_of(PACK + t), total_banks)
             if t == 0:
-                place(sup_pages[last_pages], sup_list, h1_planes[last], wg1_dealt[:, last, :])
+                place(last_sup, sup_list, h1_planes[last], wg1_dealt[last][:])
             for half in range(HALVES):
                 back = banks[((1, 2), (7, 0), (1, 2))[t][half]]
                 turn_back(total_banks[half], ACT.Tanh, [back[:, b * P : (b + 1) * P] for b in range(4)])
@@ -413,7 +428,7 @@ def tile_list_surplus_exchange_slots_kernel(
                             z_pairs[m0][:, t // 2, :, t % 2], back[:, c0 : c0 + width],
                             ACT.Copy, scale=gain_sb[:, 1, t : t + 1],
                         )
-        add_turned([standing[4 + last], sup_pages[last_pages]], pairs[1])
+        add_turned([standing[PACK + last], last_sup], pairs[1])
         partial = pairs[0]
         for half in range(HALVES):
             turn_back(pairs[1][half], ACT.Copy, [partial[half][:, b * P : (b + 1) * P] for b in range(4)])
@@ -442,8 +457,7 @@ def tile_list_surplus_exchange_slots_kernel(
 
         for g in range(EARLY_GROUPS):
             dispatch_pass(0, g)
-        last_page = dem_pages[last_pages]
-        place(last_page, dem_list, h2_planes[last], wg2_dealt[:, last, :])
+        place(last_page, dem_list, h2_planes[last], wg2_dealt[last][:])
         for m0, width in CHUNKS:
             half, c0 = divmod(m0, BANK)
             total = kept([P, width], F32, f"total{m0}")

@@ -76,7 +76,7 @@ def tile_list_surplus_exchange_slots_kernel(
                 )
 
         tab_plane = placed([P, T], U8, "tab_plane", LOTS_AT + KIB)
-        zero(tab_plane, nc.vector)
+        zero(tab_plane, nc.gpsimd)
         wsup_plane_early = placed([P, K_PASSES * EARLY_COLS], U8, "wsup_plane_early", WOVEN_AT + 4 * KIB)
         zero(wsup_plane_early, nc.gpsimd)
         lot_planes = [kept([P, S], U8, f"lot_plane{a}") for a in range(K_PASSES)]
@@ -100,20 +100,16 @@ def tile_list_surplus_exchange_slots_kernel(
             return tile
 
         load_tab(0)
+        lot_list = load_list(offs, "lot_list")
         for quad in range(4):
-            nc.scalar.dma_start(
+            (nc.sync if quad < 2 else nc.scalar).dma_start(
                 tab_plane[32 * quad : 32 * quad + 4 * K_PASSES, :].bitcast(I32),
                 tab_scales[:, 4 * quad : 4 * quad + 4, :].bitcast(I32),
             )
-        load_scale_rows(wsup_plane_early, wsup_scales, slice(0, EARLY_COLS), nc.scalar)
-        lot_list = load_list(offs, "lot_list")
         load_tab(1)
-        wsup_first = load_wsup(placed([P, K_PASSES, 2 * P], U8, "wsup_first", WOVEN_AT + 2 * KIB - 384), 0, P)
-        sup_list = load_list(offs2, "sup_list")
         load_tab(2)
-        wg1_sb = keep.tile([P, S], F32, name="wg1_sb")
-        nc.sync.dma_start(wg1_sb[:], wg1)
-        wsup_mid = load_wsup(kept([P, K_PASSES, 2 * (K_PASS - P)], U8, "wsup_mid"), P, K_PASS)
+        wsup_first = load_wsup(placed([P, K_PASSES, 2 * P], U8, "wsup_first", WOVEN_AT + 2 * KIB - 384), 0, P)
+        load_scale_rows(wsup_plane_early, wsup_scales, slice(0, EARLY_COLS), nc.sync)
 
         lot_words = [
             kept([P, S], U32, "lot_words0"),
@@ -126,6 +122,10 @@ def tile_list_surplus_exchange_slots_kernel(
             nc.scalar.dma_start(
                 lot_planes[a][:LIVE_ROWS, :].bitcast(I32), lot_planes[0][4 * a : 4 * a + LIVE_ROWS, :].bitcast(I32)
             )
+        wg1_sb = keep.tile([P, S], F32, name="wg1_sb")
+        nc.sync.dma_start(wg1_sb[:], wg1)
+        sup_list = load_list(offs2, "sup_list")
+        wsup_mid = load_wsup(kept([P, K_PASSES, 2 * (K_PASS - P)], U8, "wsup_mid"), P, K_PASS)
         for a in range(1, K_PASSES):
             nc.vector.tensor_copy(lot_words[a][:], tab_tiles[a][:].indirect(lot_list[:]))
 
@@ -277,8 +277,9 @@ def tile_list_surplus_exchange_slots_kernel(
         z_codes = {}
         z_planes = {}
 
-        def quantize_z(a, m0, width, woven):
-            codes = kept([P, width], U32, f"z_codes{a}_{m0}")
+        def quantize_z(a, m0, width, woven, codes=None):
+            if codes is None:
+                codes = kept([P, width], U32, f"z_codes{a}_{m0}")
             plane = kept([P, width], U8, f"z_plane{a}_{m0}")
             nc.vector.quantize_mx(
                 out=codes[:].bitcast(FP8X4), scales=plane[:], in_=woven[:].rearrange("p m t -> p (m t)")
@@ -391,6 +392,7 @@ def tile_list_surplus_exchange_slots_kernel(
             place_plane(t)
 
         z0_banks = (7, 0, 1, 2, 7, 0, 5, 6)
+        z0_woven = []
         for half in range(HALVES):
             rows = placed([P, 2, BANK, 2], BF16, f"z0_pairs{half}", RAW_LATE_AT + 4 * half * KIB)
             for t in range(PACK):
@@ -400,7 +402,8 @@ def tile_list_surplus_exchange_slots_kernel(
                 nc.scalar.activation(rows[:, t // 2, :, t % 2], back[:], ACT.Copy, scale=gain_sb[:, 0, t : t + 1])
             woven = placed([P, BANK, PACK], BF16, f"z0_woven{half}", RAW_LATE_AT + (8 + 4 * half) * KIB)
             nc.scalar.copy(woven_words(woven, U32), words_of(rows, U32))
-            quantize_z(0, half * BANK, BANK, woven)
+            z0_woven.append(woven)
+        quantize_z(0, 0, BANK, z0_woven[0])
         last = PACK - 1
         h1_last = placed([P, S], F32, "h1_last", RAW_LATE_AT + 4 * KIB)
         h1_planes.append(supply_plane(sup_turned, last, h1_last[:]))
@@ -471,12 +474,14 @@ def tile_list_surplus_exchange_slots_kernel(
             woven = placed([P, width, PACK], BF16, f"z1_woven{m0}", TAB_AT + 8 * m0)
             nc.vector.tensor_copy(woven_words(woven, I32), words_of(z_pairs[m0], I32))
             quantize_z(1, m0, width, woven)
+            if m0 == 128:
+                quantize_z(0, BANK, BANK, z0_woven[1], placed([P, BANK], U32, "z_codes_late", TAB_AT))
         for g in range(len(parts)):
             if g >= EARLY_GROUPS:
                 dispatch_pass(0, g)
             dispatch_pass(1, g)
             result = score_tile()
-            if g in (6, 8, 10):
+            if g in (3, 5, 7, 9, 11):
                 nc.vector.tensor_copy(result[:], banks[bank_order[g]][:])
             else:
                 nc.scalar.copy(result[:], banks[bank_order[g]][:])

@@ -141,9 +141,9 @@ def tile_list_surplus_exchange_slots_kernel(
 
         zeroed_page("dem_page0", TAB_AT + 14 * KIB)
         zeroed_page("dem_page1", TAB_AT + 18 * KIB)
-        ident = placed([P, P], F32, "ident", TAB_AT + 22 * KIB)
+        ident = keep.tile([P, P], F32, name="ident")
         make_identity(nc, ident[:])
-        zeroed_page("dem_page2", TAB_AT + 22 * KIB + 4 * P)
+        zeroed_page("dem_page2", TAB_AT + 22 * KIB)
         wdis_plane = placed([P, R_PASSES * N], U8, "wdis_plane", TAB_AT + 12 * KIB)
         zero(wdis_plane, nc.gpsimd)
 
@@ -177,11 +177,9 @@ def tile_list_surplus_exchange_slots_kernel(
             nc.scalar.copy(h1, acc[:])
             return h1
 
-        def supply_turned(words):
-            turned = placed([P, S // P, PACK, P], F32, "turned", TAB_AT)
+        def supply_turned(words, turned, blocks, accs):
             s0 = K_PASS - EARLY_COLS
-            for jb in range(S // P):
-                acc = next_acc()
+            for jb, acc in zip(blocks, accs):
                 for a in range(K_PASSES):
                     nc.tensor.matmul_mx(
                         out=acc[:],
@@ -193,7 +191,6 @@ def tile_list_surplus_exchange_slots_kernel(
                         stop=(a == K_PASSES - 1),
                     )
                 nc.scalar.copy(turned[:, jb], acc[:].rearrange("j (p t) -> j t p", t=PACK))
-            return turned
 
         def supply_plane(turned, t, h1):
             acc = next_acc()
@@ -334,13 +331,15 @@ def tile_list_surplus_exchange_slots_kernel(
         dem_list = load_list(offs3, "dem_list")
         wg2_sb = keep.tile([P, S], F32, name="wg2_sb")
         nc.sync.dma_start(wg2_sb[:], wg2)
-        standing = [load_standing(stand[0:P, :])]
-        for i in range(2):
-            place(dem_pages[i], dem_list, demand(i, score_tile()[:], next_acc()), wg2_sb[:])
-        h1_tile3 = supply(3, quantize_quarter(1, (16, 20, 4)), banks[7])
         load_scale_rows(wsup_plane_late, wsup_scales, slice(EARLY_COLS, H), nc.sync)
         wsup_late = load_wsup(kept([P, K_PASSES, 2 * K_PASS], U8, "wsup_late"), K_PASS, H)
-        sup_turned = supply_turned(wsup_late)
+        sup_turned = placed([P, S // P, PACK, P], F32, "turned", TAB_AT)
+        supply_turned(wsup_late, sup_turned, (0, 1), pairs[1])
+        standing = [load_standing(stand[0:P, :])]
+        for i in range(2):
+            place(dem_pages[i], dem_list, demand(i, score_tile()[:], banks[i]), wg2_sb[:])
+        supply_turned(wsup_late, sup_turned, (2, 3), banks[:2])
+        h1_tile3 = supply(3, quantize_quarter(1, (16, 20, 4)), banks[7])
         bound_tile(0)
         place(sup_pages[0], sup_list, h1_tile3, wg1_sb[:])
         quantize_late(0)
@@ -480,13 +479,21 @@ def tile_list_surplus_exchange_slots_kernel(
             if g >= EARLY_GROUPS:
                 dispatch_pass(0, g)
             dispatch_pass(1, g)
-            result = score_tile()
-            if g in (3, 5, 7, 9, 11):
-                nc.vector.tensor_copy(result[:], banks[bank_order[g]][:])
-            else:
-                nc.scalar.copy(result[:], banks[bank_order[g]][:])
             m0, j0 = parts[g][0]
+            if g < EARLY_GROUPS:
+                result = score_tile()[:]
+            else:
+                if j0 % 2 == 0:
+                    both = placed([P, 2, BANK], F32, f"result{g}", RAW_AT + (0, 16, 20)[j0 // 2] * KIB)
+                result = both[:, j0 % 2, :]
+            if g in (3, 5, 7, 9, 11):
+                nc.vector.tensor_copy(result, banks[bank_order[g]][:])
+            else:
+                nc.scalar.copy(result, banks[bank_order[g]][:])
             tiles = parts[g][-1][1] - j0 + 1
-            nc.sync.dma_start(
-                out_rows[:, j0 : j0 + tiles, m0 : m0 + BANK // tiles], result[:].rearrange("p (j m) -> p j m", j=tiles)
-            )
+            if g < EARLY_GROUPS:
+                nc.sync.dma_start(
+                    out_rows[:, j0 : j0 + tiles, m0 : m0 + BANK // tiles], result.rearrange("p (j m) -> p j m", j=tiles)
+                )
+            elif j0 % 2 == 1:
+                nc.sync.dma_start(out_rows[:, j0 - 1 : j0 + 1, m0 : m0 + BANK], both[:])

@@ -29,11 +29,14 @@ HALVES = T2 // BANK
 QUARTER = 256
 SUP_PAGES = 3
 DEM_PAGES = 3
+FIRST_COLS = 2 * P
 EARLY_COLS = 4 * P
 LIVE_ROWS = 100
 KIB = 1024
 CHUNKS = ((0, 128), (128, 128), (256, 256), (512, 512))
 EARLY_GROUPS = 6
+LATE_N = 4 * P
+WARM_UPS = 4
 
 TAB_AT = 0
 LOTS_AT = 27 * KIB
@@ -108,7 +111,7 @@ def tile_list_surplus_exchange_slots_kernel(
             )
         load_tab(1)
         load_tab(2)
-        wsup_first = load_wsup(placed([P, K_PASSES, 2 * P], U8, "wsup_first", WOVEN_AT + 2 * KIB - 384), 0, P)
+        wsup_first = load_wsup(placed([P, K_PASSES, 2 * FIRST_COLS], U8, "wsup_first", WOVEN_AT + 2 * KIB - 768), 0, FIRST_COLS)
         load_scale_rows(wsup_plane_early, wsup_scales, slice(0, EARLY_COLS), nc.sync)
 
         lot_words = [
@@ -125,7 +128,7 @@ def tile_list_surplus_exchange_slots_kernel(
         wg1_sb = keep.tile([P, S], F32, name="wg1_sb")
         nc.sync.dma_start(wg1_sb[:], wg1)
         sup_list = load_list(offs2, "sup_list")
-        wsup_mid = load_wsup(kept([P, K_PASSES, 2 * (K_PASS - P)], U8, "wsup_mid"), P, K_PASS)
+        wsup_mid = load_wsup(kept([P, K_PASSES, 2 * (K_PASS - FIRST_COLS)], U8, "wsup_mid"), FIRST_COLS, K_PASS)
         for a in range(1, K_PASSES):
             nc.vector.tensor_copy(lot_words[a][:], tab_tiles[a][:].indirect(lot_list[:]))
 
@@ -159,20 +162,21 @@ def tile_list_surplus_exchange_slots_kernel(
             return ring.tile([P, S], F32, name="scores", tag="scores", bufs=12)
 
         def supply(i, h1, acc):
-            words, c0 = (wsup_first, 0) if i == 0 else (wsup_mid, (i - 1) * P)
+            words, c0 = (wsup_first, i * P) if i * P < FIRST_COLS else (wsup_mid, i * P - FIRST_COLS)
+            order = (0, 1, 2) if i == 0 else (2, 0, 1)
             if i * P < EARLY_COLS:
                 plane, width, s0 = wsup_plane_early, EARLY_COLS, i * P
             else:
                 plane, width, s0 = wsup_plane_late, late_cols, i * P - EARLY_COLS
-            for a in range(K_PASSES):
+            for a in order:
                 nc.tensor.matmul_mx(
                     out=acc[:],
                     lhsT=words[:, a, 2 * c0 : 2 * (c0 + P)].bitcast(FP4X4),
                     lhsT_scale=plane[:, a * width + s0 : a * width + s0 + P],
                     rhs=lot_words[a][:].bitcast(FP8X4),
                     rhs_scale=lot_planes[a][:],
-                    start=(a == 0),
-                    stop=(a == K_PASSES - 1),
+                    start=(a == order[0]),
+                    stop=(a == order[-1]),
                 )
             nc.scalar.copy(h1, acc[:])
             return h1
@@ -310,6 +314,16 @@ def tile_list_surplus_exchange_slots_kernel(
                     ACT.Tanh,
                 )
 
+        for warm in range(WARM_UPS):
+            nc.tensor.matmul_mx(
+                out=banks[6][:],
+                lhsT=lot_words[0][:, :P].bitcast(FP8X4),
+                lhsT_scale=lot_planes[0][:, :P],
+                rhs=lot_words[0][:].bitcast(FP8X4),
+                rhs_scale=lot_planes[0][:],
+                start=True,
+                stop=True,
+            )
         for i in range(2):
             place(sup_pages[i], sup_list, supply(i, score_tile()[:], next_acc()), wg1_sb[:])
 
@@ -383,8 +397,9 @@ def tile_list_surplus_exchange_slots_kernel(
         standing.append(load_standing(stand_planes[:, 0, :]))
         standing.append(load_standing(stand_planes[:, 1, :]))
         load_dealt(3)
-        wdis_sb = kept([P, R_PASSES, N], U32, "wdis_sb")
-        nc.sync.dma_start(wdis_sb[:].bitcast(I32), wdis_words.rearrange("a p c i -> p a (c i)").bitcast(I32))
+        wdis_rows = wdis_words.rearrange("a p c i -> p a (c i)").bitcast(I32)
+        wdis_sb = kept([P, R_PASSES, LATE_N], U32, "wdis_sb")
+        nc.sync.dma_start(wdis_sb[:].bitcast(I32), wdis_rows[:, :, :LATE_N])
         load_scale_rows(wdis_plane, wdis_scales, slice(0, N), nc.sync)
 
         for t in range(PACK - 1):
@@ -402,7 +417,8 @@ def tile_list_surplus_exchange_slots_kernel(
             woven = placed([P, BANK, PACK], BF16, f"z0_woven{half}", RAW_LATE_AT + (8 + 4 * half) * KIB)
             nc.scalar.copy(woven_words(woven, U32), words_of(rows, U32))
             z0_woven.append(woven)
-        quantize_z(0, 0, BANK, z0_woven[0])
+        for half in range(HALVES):
+            quantize_z(0, half * BANK, BANK, z0_woven[half])
         last = PACK - 1
         h1_last = placed([P, S], F32, "h1_last", RAW_LATE_AT + 4 * KIB)
         h1_planes.append(supply_plane(sup_turned, last, h1_last[:]))
@@ -435,6 +451,8 @@ def tile_list_surplus_exchange_slots_kernel(
         for half in range(HALVES):
             turn_back(pairs[1][half], ACT.Copy, [partial[half][:, b * P : (b + 1) * P] for b in range(4)])
 
+        wdis_late = placed([P, R_PASSES, N - LATE_N], U32, "wdis_late", RAW_LATE_AT + 4 * KIB)
+        nc.sync.dma_start(wdis_late[:].bitcast(I32), wdis_rows[:, :, LATE_N:])
         out_rows = out.rearrange("(j p) m -> p j m", p=P)
         bank_order = (7, 0, 1, 2, 5, 6, 3, 4, 7, 0, 1, 2)
         parts = [
@@ -447,9 +465,10 @@ def tile_list_surplus_exchange_slots_kernel(
             acc = banks[bank_order[g]]
             for n_part, (m0, j) in enumerate(parts[g]):
                 width = widths[m0]
+                words, n0 = (wdis_sb, j * P) if j * P < LATE_N else (wdis_late, j * P - LATE_N)
                 nc.tensor.matmul_mx(
                     out=acc[:, n_part * width : (n_part + 1) * width],
-                    lhsT=wdis_sb[:, a, j * P : (j + 1) * P].bitcast(FP8X4),
+                    lhsT=words[:, a, n0 : n0 + P].bitcast(FP8X4),
                     lhsT_scale=wdis_plane[:, a * N + j * P : a * N + (j + 1) * P],
                     rhs=z_codes[a, m0].bitcast(FP8X4),
                     rhs_scale=z_planes[a, m0],
@@ -473,8 +492,6 @@ def tile_list_surplus_exchange_slots_kernel(
             woven = placed([P, width, PACK], BF16, f"z1_woven{m0}", TAB_AT + 8 * m0)
             nc.vector.tensor_copy(woven_words(woven, I32), words_of(z_pairs[m0], I32))
             quantize_z(1, m0, width, woven)
-            if m0 == 128:
-                quantize_z(0, BANK, BANK, z0_woven[1], placed([P, BANK], U32, "z_codes_late", TAB_AT))
         for g in range(len(parts)):
             if g >= EARLY_GROUPS:
                 dispatch_pass(0, g)

@@ -36,7 +36,6 @@ KIB = 1024
 CHUNKS = ((0, 128), (128, 128), (256, 256), (512, 512))
 EARLY_GROUPS = 6
 LATE_N = 4 * P
-WARM_UPS = 4
 
 TAB_AT = 0
 LOTS_AT = 27 * KIB
@@ -314,16 +313,6 @@ def tile_list_surplus_exchange_slots_kernel(
                     ACT.Tanh,
                 )
 
-        for warm in range(WARM_UPS):
-            nc.tensor.matmul_mx(
-                out=banks[6][:],
-                lhsT=lot_words[0][:, :P].bitcast(FP8X4),
-                lhsT_scale=lot_planes[0][:, :P],
-                rhs=lot_words[0][:].bitcast(FP8X4),
-                rhs_scale=lot_planes[0][:],
-                start=True,
-                stop=True,
-            )
         for i in range(2):
             place(sup_pages[i], sup_list, supply(i, score_tile()[:], next_acc()), wg1_sb[:])
 

@@ -33,15 +33,17 @@ FIRST_COLS = 2 * P
 EARLY_COLS = 4 * P
 LIVE_ROWS = 100
 KIB = 1024
+PIECES = (((0, 128),), ((128, 128), (256, 256)))
 CHUNKS = ((0, 128), (128, 128), (256, 256), (512, 512))
 EARLY_GROUPS = 6
 LATE_N = 4 * P
 
 TAB_AT = 0
-LOTS_AT = 27 * KIB
-WOVEN_AT = 31 * KIB
-RAW_AT = 37 * KIB
-RAW_LATE_AT = 61 * KIB
+WOVEN_AT = 26 * KIB
+RAW_AT = 36 * KIB
+MID_AT = RAW_AT + 8 * KIB - 1536
+RAW_LATE_AT = RAW_AT + 24 * KIB
+TURNED_AT = RAW_LATE_AT + 24 * KIB
 
 
 def tile_list_surplus_exchange_slots_kernel(
@@ -77,7 +79,7 @@ def tile_list_surplus_exchange_slots_kernel(
                     source[:, 4 * quad : 4 * quad + 4, cols].rearrange("a r c -> r a c").bitcast(I32),
                 )
 
-        tab_plane = placed([P, T], U8, "tab_plane", LOTS_AT + KIB)
+        tab_plane = placed([P, T], U8, "tab_plane", MID_AT - 64)
         zero(tab_plane, nc.gpsimd)
         wsup_plane_early = placed([P, K_PASSES * EARLY_COLS], U8, "wsup_plane_early", WOVEN_AT + 4 * KIB)
         zero(wsup_plane_early, nc.gpsimd)
@@ -109,27 +111,30 @@ def tile_list_surplus_exchange_slots_kernel(
                 tab_scales[:, 4 * quad : 4 * quad + 4, :].bitcast(I32),
             )
         load_tab(1)
-        load_tab(2)
         wsup_first = load_wsup(placed([P, K_PASSES, 2 * FIRST_COLS], U8, "wsup_first", WOVEN_AT + 2 * KIB - 768), 0, FIRST_COLS)
-        load_scale_rows(wsup_plane_early, wsup_scales, slice(0, EARLY_COLS), nc.sync)
+        load_tab(2)
+        sup_list = load_list(offs2, "sup_list")
+        dem_list = load_list(offs3, "dem_list")
+        load_scale_rows(wsup_plane_early, wsup_scales, slice(0, EARLY_COLS), nc.gpsimd)
 
-        lot_words = [
-            kept([P, S], U32, "lot_words0"),
-            placed([P, S], U32, "lot_words1", LOTS_AT),
-            placed([P, S], U32, "lot_words2", LOTS_AT + 2 * KIB),
-        ]
+        lot_words = [kept([P, S], U32, f"lot_words{a}") for a in range(K_PASSES)]
         nc.vector.tensor_copy(lot_words[0][:], tab_tiles[0][:].indirect(lot_list[:]))
         nc.vector.tensor_copy(lot_planes[0][:], tab_plane[:].indirect(lot_list[:]))
         for a in range(1, K_PASSES):
-            nc.scalar.dma_start(
+            nc.sync.dma_start(
                 lot_planes[a][:LIVE_ROWS, :].bitcast(I32), lot_planes[0][4 * a : 4 * a + LIVE_ROWS, :].bitcast(I32)
             )
-        wg1_sb = keep.tile([P, S], F32, name="wg1_sb")
+        wg1_sb = placed([P, S], F32, "wg1_sb", MID_AT - 2 * KIB)
         nc.sync.dma_start(wg1_sb[:], wg1)
-        sup_list = load_list(offs2, "sup_list")
-        wsup_mid = load_wsup(kept([P, K_PASSES, 2 * (K_PASS - FIRST_COLS)], U8, "wsup_mid"), FIRST_COLS, K_PASS)
-        for a in range(1, K_PASSES):
-            nc.vector.tensor_copy(lot_words[a][:], tab_tiles[a][:].indirect(lot_list[:]))
+        wsup_mid = load_wsup(placed([P, K_PASSES, 2 * (K_PASS - FIRST_COLS)], U8, "wsup_mid", MID_AT), FIRST_COLS, K_PASS)
+
+        def span(piece):
+            return piece[0][0], piece[-1][0] + piece[-1][1]
+
+        nc.vector.tensor_copy(lot_words[1][:], tab_tiles[1][:].indirect(lot_list[:]))
+        for piece in PIECES:
+            j0, j1 = span(piece)
+            nc.vector.tensor_copy(lot_words[2][:, j0:j1], tab_tiles[2][:].indirect(lot_list[:, j0 // 16 : j1 // 16]))
 
         late_cols = H - EARLY_COLS
         wsup_plane_late = placed([P, K_PASSES * late_cols], U8, "wsup_plane_late", TAB_AT + 8 * KIB)
@@ -155,29 +160,27 @@ def tile_list_surplus_exchange_slots_kernel(
 
         def next_acc():
             acc_turn.append(None)
-            return banks[(len(acc_turn) - 1) % 3]
+            return banks[(len(acc_turn) + 1) % 3]
 
         def score_tile():
             return ring.tile([P, S], F32, name="scores", tag="scores", bufs=12)
 
-        def supply(i, h1, acc):
+        def supply(i, h1, acc, piece=((0, S),)):
             words, c0 = (wsup_first, i * P) if i * P < FIRST_COLS else (wsup_mid, i * P - FIRST_COLS)
-            order = (0, 1, 2) if i == 0 else (2, 0, 1)
-            if i * P < EARLY_COLS:
-                plane, width, s0 = wsup_plane_early, EARLY_COLS, i * P
-            else:
-                plane, width, s0 = wsup_plane_late, late_cols, i * P - EARLY_COLS
+            j0, j1 = span(piece)
+            order = (0, 1, 2) if j1 == P else (2, 0, 1)
             for a in order:
-                nc.tensor.matmul_mx(
-                    out=acc[:],
-                    lhsT=words[:, a, 2 * c0 : 2 * (c0 + P)].bitcast(FP4X4),
-                    lhsT_scale=plane[:, a * width + s0 : a * width + s0 + P],
-                    rhs=lot_words[a][:].bitcast(FP8X4),
-                    rhs_scale=lot_planes[a][:],
-                    start=(a == order[0]),
-                    stop=(a == order[-1]),
-                )
-            nc.scalar.copy(h1, acc[:])
+                for n_part, (j, width) in enumerate(piece):
+                    nc.tensor.matmul_mx(
+                        out=acc[:, j - j0 : j - j0 + width],
+                        lhsT=words[:, a, 2 * c0 : 2 * (c0 + P)].bitcast(FP4X4),
+                        lhsT_scale=wsup_plane_early[:, a * EARLY_COLS + i * P : a * EARLY_COLS + (i + 1) * P],
+                        rhs=lot_words[a][:, j : j + width].bitcast(FP8X4),
+                        rhs_scale=lot_planes[a][:, j : j + width],
+                        start=(a == order[0] and n_part == 0),
+                        stop=(a == order[-1] and n_part == len(piece) - 1),
+                    )
+            nc.scalar.copy(h1[:, j0:j1], acc[:, : j1 - j0])
             return h1
 
         def supply_turned(words, turned, blocks, accs):
@@ -247,8 +250,10 @@ def tile_list_surplus_exchange_slots_kernel(
             nc.scalar.activation(h2, acc[:], ACT.Copy, scale=-1.0)
             return h2
 
-        def place(page, slots, scores, weights):
-            nc.vector.tensor_tensor(page[:].indirect(slots[:]), scores, weights, MULT)
+        def place(page, slots, scores, weights, j0=0, j1=S):
+            nc.vector.tensor_tensor(
+                page[:].indirect(slots[:, j0 // 16 : j1 // 16]), scores[:, j0:j1], weights[:, j0:j1], MULT
+            )
 
         def load_standing(rows, tile=None):
             if tile is None:
@@ -313,11 +318,14 @@ def tile_list_surplus_exchange_slots_kernel(
                     ACT.Tanh,
                 )
 
-        for i in range(2):
-            place(sup_pages[i], sup_list, supply(i, score_tile()[:], next_acc()), wg1_sb[:])
+        first_scores = [score_tile()[:] for i in range(2)]
+        for n_piece, piece in enumerate(PIECES):
+            for i in range(2):
+                supply(i, first_scores[i], pairs[n_piece][i], piece)
+                place(sup_pages[i], sup_list, first_scores[i], wg1_sb[:], *span(piece))
 
         def quantize_quarter(quarter, raw_at):
-            raws = [load_wdem(a, quarter * QUARTER, QUARTER, RAW_AT + raw_at[a] * KIB) for a in range(K_PASSES)]
+            raws = [load_wdem(a, quarter * QUARTER, QUARTER, raw_at[a]) for a in range(K_PASSES)]
             for a in range(K_PASSES):
                 woven = placed([P, QUARTER, PACK], BF16, f"woven{a}_{quarter}", WOVEN_AT + 2 * a * KIB)
                 quantize_wdem(a, quarter * QUARTER, raws[a], woven)
@@ -330,19 +338,18 @@ def tile_list_surplus_exchange_slots_kernel(
             woven = ring.tile([P, K_PASS, PACK], BF16, name="woven", tag="woven", bufs=3, align_bytes=64)
             quantize_wdem(a, K_PASS, late_raws[a], woven)
 
-        place(sup_pages[2], sup_list, supply(2, quantize_quarter(0, (8, 12, 0)), next_acc()), wg1_sb[:])
-        dem_list = load_list(offs3, "dem_list")
+        place(sup_pages[2], sup_list, supply(2, quantize_quarter(0, (RAW_AT + 8 * KIB, TAB_AT, TAB_AT + 4 * KIB)), next_acc()), wg1_sb[:])
         wg2_sb = keep.tile([P, S], F32, name="wg2_sb")
         nc.sync.dma_start(wg2_sb[:], wg2)
         load_scale_rows(wsup_plane_late, wsup_scales, slice(EARLY_COLS, H), nc.sync)
         wsup_late = load_wsup(kept([P, K_PASSES, 2 * K_PASS], U8, "wsup_late"), K_PASS, H)
-        sup_turned = placed([P, S // P, PACK, P], F32, "turned", TAB_AT)
+        sup_turned = placed([P, S // P, PACK, P], F32, "turned", TURNED_AT)
         supply_turned(wsup_late, sup_turned, (0, 1), pairs[1])
         standing = [load_standing(stand[0:P, :])]
         for i in range(2):
             place(dem_pages[i], dem_list, demand(i, score_tile()[:], banks[i]), wg2_sb[:])
         supply_turned(wsup_late, sup_turned, (2, 3), banks[:2])
-        h1_tile3 = supply(3, quantize_quarter(1, (16, 20, 4)), banks[7])
+        h1_tile3 = supply(3, quantize_quarter(1, (RAW_AT + 16 * KIB, RAW_AT + 20 * KIB, RAW_AT)), banks[7])
         bound_tile(0)
         place(sup_pages[0], sup_list, h1_tile3, wg1_sb[:])
         quantize_late(0)

@@ -451,9 +451,7 @@ def tile_list_surplus_exchange_slots_kernel(
         nc.sync.dma_start(wdis_late[:].bitcast(I32), wdis_rows[:, :, LATE_N:])
         out_rows = out.rearrange("(j p) m -> p j m", p=P)
         bank_order = (7, 0, 1, 2, 5, 6, 3, 4, 7, 0, 1, 2)
-        parts = [
-            [(0, j) for j in range(4)], [(128, j) for j in range(4)], [(0, 4), (128, 4), (0, 5), (128, 5)],
-        ]
+        parts = [[(0, j), (0, j + 1), (128, j), (128, j + 1)] for j in range(0, 6, 2)]
         parts = parts + [[(256, j), (256, j + 1)] for j in range(0, 6, 2)] + [[(512, j)] for j in range(6)]
         widths = dict(CHUNKS)
 
@@ -462,8 +460,9 @@ def tile_list_surplus_exchange_slots_kernel(
             for n_part, (m0, j) in enumerate(parts[g]):
                 width = widths[m0]
                 words, n0 = (wdis_sb, j * P) if j * P < LATE_N else (wdis_late, j * P - LATE_N)
+                at = (j - parts[g][0][1]) * QUARTER + m0 - parts[g][0][0]
                 nc.tensor.matmul_mx(
-                    out=acc[:, n_part * width : (n_part + 1) * width],
+                    out=acc[:, at : at + width],
                     lhsT=words[:, a, n0 : n0 + P].bitcast(FP8X4),
                     lhsT_scale=wdis_plane[:, a * N + j * P : a * N + (j + 1) * P],
                     rhs=z_codes[a, m0].bitcast(FP8X4),
@@ -481,10 +480,7 @@ def tile_list_surplus_exchange_slots_kernel(
             nc.vector.tensor_tensor(total[:], partial[half][:, c0 : c0 + width], last_page[:, m0 : m0 + width], ADD)
             squashed = kept([P, width], F32, f"squashed{m0}")
             nc.scalar.activation(squashed[:], total[:], ACT.Tanh)
-            nc.scalar.activation(
-                z_pairs[m0][:, 1, :, 1], squashed[:], ACT.Copy, scale=gain_sb[:, 1, last : last + 1]
-            )
-        for m0, width in CHUNKS:
+            nc.vector.tensor_scalar(z_pairs[m0][:, 1, :, 1], squashed[:], gain_sb[:, 1, last : last + 1], None, MULT)
             woven = placed([P, width, PACK], BF16, f"z1_woven{m0}", TAB_AT + 8 * m0)
             nc.vector.tensor_copy(woven_words(woven, I32), words_of(z_pairs[m0], I32))
             quantize_z(1, m0, width, woven)
@@ -499,7 +495,7 @@ def tile_list_surplus_exchange_slots_kernel(
                 if j0 % 2 == 0:
                     both = placed([P, 2, BANK], F32, f"result{g}", RAW_AT + (0, 16, 20)[j0 // 2] * KIB)
                 result = both[:, j0 % 2, :]
-            if g in (3, 5, 7, 9, 11):
+            if g in (7, 9, 11):
                 nc.vector.tensor_copy(result, banks[bank_order[g]][:])
             else:
                 nc.scalar.copy(result, banks[bank_order[g]][:])

@@ -413,11 +413,12 @@ def tile_list_surplus_exchange_slots_kernel(
             woven = placed([P, BANK, PACK], BF16, f"z0_woven{half}", RAW_LATE_AT + (8 + 4 * half) * KIB)
             nc.scalar.copy(woven_words(woven, U32), words_of(rows, U32))
             z0_woven.append(woven)
+            if half == 0:
+                h1_last = placed([P, S], F32, "h1_last", RAW_LATE_AT)
+                h1_planes.append(supply_plane(sup_turned, PACK - 1, h1_last[:]))
         for half in range(HALVES):
             quantize_z(0, half * BANK, BANK, z0_woven[half])
         last = PACK - 1
-        h1_last = placed([P, S], F32, "h1_last", RAW_LATE_AT + 4 * KIB)
-        h1_planes.append(supply_plane(sup_turned, last, h1_last[:]))
         h2_last = placed([P, S], F32, "h2_last", RAW_LATE_AT + 6 * KIB)
         h2_planes.append(demand(PACK + last, h2_last[:], next_acc()))
         for t in range(2, PACK):
@@ -442,15 +443,15 @@ def tile_list_surplus_exchange_slots_kernel(
                             z_pairs[m0][:, t // 2, :, t % 2], back[:, c0 : c0 + width],
                             ACT.Copy, scale=gain_sb[:, 1, t : t + 1],
                         )
-        add_turned([standing[PACK + last], last_sup], pairs[1])
-        partial = pairs[0]
+        add_turned([standing[PACK + last], last_sup], pairs[0])
+        partial = pairs[1]
         for half in range(HALVES):
-            turn_back(pairs[1][half], ACT.Copy, [partial[half][:, b * P : (b + 1) * P] for b in range(4)])
+            turn_back(pairs[0][half], ACT.Copy, [partial[half][:, b * P : (b + 1) * P] for b in range(4)])
 
-        wdis_late = placed([P, R_PASSES, N - LATE_N], U32, "wdis_late", RAW_LATE_AT + 4 * KIB)
+        wdis_late = placed([P, R_PASSES, N - LATE_N], U32, "wdis_late", RAW_LATE_AT)
         nc.sync.dma_start(wdis_late[:].bitcast(I32), wdis_rows[:, :, LATE_N:])
         out_rows = out.rearrange("(j p) m -> p j m", p=P)
-        bank_order = (7, 0, 1, 2, 5, 6, 3, 4, 7, 0, 1, 2)
+        bank_order = (7, 0, 1, 2, 3, 4, 5, 6, 7, 0, 1, 2)
         parts = [[(0, j), (0, j + 1), (128, j), (128, j + 1)] for j in range(0, 6, 2)]
         parts = parts + [[(256, j), (256, j + 1)] for j in range(0, 6, 2)] + [[(512, j)] for j in range(6)]
         widths = dict(CHUNKS)

@@ -40,6 +40,7 @@ LATE_N = 4 * P
 
 TAB_AT = 0
 WOVEN_AT = 26 * KIB
+SPARE_AT = 32 * KIB
 RAW_AT = 36 * KIB
 MID_AT = RAW_AT + 8 * KIB - 1536
 RAW_LATE_AT = RAW_AT + 24 * KIB
@@ -324,11 +325,11 @@ def tile_list_surplus_exchange_slots_kernel(
                 supply(i, first_scores[i], pairs[n_piece][i], piece)
                 place(sup_pages[i], sup_list, first_scores[i], wg1_sb[:], *span(piece))
 
-        def quantize_quarter(quarter, raw_at):
-            raws = [load_wdem(a, quarter * QUARTER, QUARTER, raw_at[a]) for a in range(K_PASSES)]
-            for a in range(K_PASSES):
-                woven = placed([P, QUARTER, PACK], BF16, f"woven{a}_{quarter}", WOVEN_AT + 2 * a * KIB)
-                quantize_wdem(a, quarter * QUARTER, raws[a], woven)
+        def quantize_quarter(quarter, passes, raw_at, woven_at):
+            raws = [load_wdem(a, quarter * QUARTER, QUARTER, at) for a, at in zip(passes, raw_at)]
+            for a, raw in zip(passes, raws):
+                woven = placed([P, QUARTER, PACK], BF16, f"woven{a}_{quarter}", woven_at + 2 * a * KIB)
+                quantize_wdem(a, quarter * QUARTER, raw, woven)
             return raws[-1][:].rearrange("p j c -> p (j c)")[:, :S]
 
         late_raws = []
@@ -338,18 +339,18 @@ def tile_list_surplus_exchange_slots_kernel(
             woven = ring.tile([P, K_PASS, PACK], BF16, name="woven", tag="woven", bufs=3, align_bytes=64)
             quantize_wdem(a, K_PASS, late_raws[a], woven)
 
-        place(sup_pages[2], sup_list, supply(2, quantize_quarter(0, (RAW_AT + 8 * KIB, TAB_AT, TAB_AT + 4 * KIB)), next_acc()), wg1_sb[:])
+        place(sup_pages[2], sup_list, supply(2, quantize_quarter(0, (0, 1, 2), (RAW_AT + 8 * KIB, TAB_AT, TAB_AT + 4 * KIB), WOVEN_AT), next_acc()), wg1_sb[:])
         wg2_sb = keep.tile([P, S], F32, name="wg2_sb")
         nc.sync.dma_start(wg2_sb[:], wg2)
+        quantize_quarter(1, (0, 1), (RAW_AT + 16 * KIB, RAW_AT + 20 * KIB), SPARE_AT)
         load_scale_rows(wsup_plane_late, wsup_scales, slice(EARLY_COLS, H), nc.sync)
         wsup_late = load_wsup(kept([P, K_PASSES, 2 * K_PASS], U8, "wsup_late"), K_PASS, H)
         sup_turned = placed([P, S // P, PACK, P], F32, "turned", TURNED_AT)
-        supply_turned(wsup_late, sup_turned, (0, 1), pairs[1])
         standing = [load_standing(stand[0:P, :])]
         for i in range(2):
             place(dem_pages[i], dem_list, demand(i, score_tile()[:], banks[i]), wg2_sb[:])
-        supply_turned(wsup_late, sup_turned, (2, 3), banks[:2])
-        h1_tile3 = supply(3, quantize_quarter(1, (RAW_AT + 16 * KIB, RAW_AT + 20 * KIB, RAW_AT)), banks[7])
+        supply_turned(wsup_late, sup_turned, range(4), pairs[1] + banks[:2])
+        h1_tile3 = supply(3, quantize_quarter(1, (2,), (RAW_AT,), WOVEN_AT), banks[7])
         bound_tile(0)
         place(sup_pages[0], sup_list, h1_tile3, wg1_sb[:])
         quantize_late(0)

@@ -36,7 +36,6 @@ KIB = 1024
 PIECES = (((0, 128),), ((128, 128), (256, 256)))
 CHUNKS = ((0, 128), (128, 128), (256, 256), (512, 512))
 EARLY_GROUPS = 6
-LATE_N = 4 * P
 
 TAB_AT = 0
 WOVEN_AT = 26 * KIB
@@ -274,8 +273,9 @@ def tile_list_surplus_exchange_slots_kernel(
                             stop=(n_term == len(terms) - 1 and b == BLOCKS_PER_BANK - 1),
                         )
 
-        def turn_back(total, func, targets):
-            turned = ring.tile([P, BANK], F32, name="turned_sum", tag="turned_sum", bufs=3)
+        def turn_back(total, func, targets, turned=None):
+            if turned is None:
+                turned = ring.tile([P, BANK], F32, name="turned_sum", tag="turned_sum", bufs=3)
             nc.scalar.activation(turned[:], total[:], func)
             for b in range(BLOCKS_PER_BANK):
                 nc.tensor.transpose(targets[b], turned[:, b * P : (b + 1) * P], ident[:])
@@ -392,11 +392,9 @@ def tile_list_surplus_exchange_slots_kernel(
         nc.sync.dma_start(gain_sb[:], gain.rearrange("(a p t) -> p a t", p=P, t=PACK))
         stand_planes = stand[K_PASS:, :].rearrange("(p t) m -> p t m", t=PACK)
         standing.append(load_standing(stand_planes[:, 0, :]))
-        standing.append(load_standing(stand_planes[:, 1, :]))
+        standing.append(load_standing(stand_planes[:, 1, :], placed([P, T2], F32, "standing1", TAB_AT)))
         load_dealt(3)
         wdis_rows = wdis_words.rearrange("a p c i -> p a (c i)").bitcast(I32)
-        wdis_sb = kept([P, R_PASSES, LATE_N], U32, "wdis_sb")
-        nc.sync.dma_start(wdis_sb[:].bitcast(I32), wdis_rows[:, :, :LATE_N])
         load_scale_rows(wdis_plane, wdis_scales, slice(0, N), nc.sync)
 
         for t in range(PACK - 1):
@@ -417,10 +415,8 @@ def tile_list_surplus_exchange_slots_kernel(
             if half == 0:
                 h1_last = placed([P, S], F32, "h1_last", RAW_LATE_AT)
                 h1_planes.append(supply_plane(sup_turned, PACK - 1, h1_last[:]))
-        for half in range(HALVES):
-            quantize_z(0, half * BANK, BANK, z0_woven[half])
         last = PACK - 1
-        h2_last = placed([P, S], F32, "h2_last", RAW_LATE_AT + 6 * KIB)
+        h2_last = placed([P, S], F32, "h2_last", TAB_AT + 2 * KIB)
         h2_planes.append(demand(PACK + last, h2_last[:], next_acc()))
         for t in range(2, PACK):
             standing.append(load_standing(stand_planes[:, t, :], placed([P, T2], F32, f"standing{t}", RAW_AT + 4 * t * KIB)))
@@ -434,9 +430,13 @@ def tile_list_surplus_exchange_slots_kernel(
             add_turned([standing[PACK + t]] + pages_of(PACK + t), total_banks)
             if t == 0:
                 place(last_sup, sup_list, h1_planes[last], wg1_dealt[last][:])
+            else:
+                codes = placed([P, BANK], U32, f"z0_codes{t - 1}", (TAB_AT, RAW_AT + 8 * KIB)[t - 1])
+                quantize_z(0, (t - 1) * BANK, BANK, z0_woven[t - 1], codes)
             for half in range(HALVES):
                 back = banks[((1, 2), (7, 0), (1, 2))[t][half]]
-                turn_back(total_banks[half], ACT.Tanh, [back[:, b * P : (b + 1) * P] for b in range(4)])
+                own = placed([P, BANK], F32, f"plane1_tanh{half}", SPARE_AT + 2 * half * KIB) if t == 1 else None
+                turn_back(total_banks[half], ACT.Tanh, [back[:, b * P : (b + 1) * P] for b in range(4)], own)
                 for m0, width in CHUNKS:
                     if m0 // BANK == half:
                         c0 = m0 % BANK
@@ -449,8 +449,8 @@ def tile_list_surplus_exchange_slots_kernel(
         for half in range(HALVES):
             turn_back(pairs[0][half], ACT.Copy, [partial[half][:, b * P : (b + 1) * P] for b in range(4)])
 
-        wdis_late = placed([P, R_PASSES, N - LATE_N], U32, "wdis_late", RAW_LATE_AT)
-        nc.sync.dma_start(wdis_late[:].bitcast(I32), wdis_rows[:, :, LATE_N:])
+        wdis_sb = placed([P, R_PASSES, N], U32, "wdis_sb", SPARE_AT - 2 * KIB)
+        nc.sync.dma_start(wdis_sb[:].bitcast(I32), wdis_rows)
         out_rows = out.rearrange("(j p) m -> p j m", p=P)
         bank_order = (7, 0, 1, 2, 3, 4, 5, 6, 7, 0, 1, 2)
         parts = [[(0, j), (0, j + 1), (128, j), (128, j + 1)] for j in range(0, 6, 2)]
@@ -461,11 +461,10 @@ def tile_list_surplus_exchange_slots_kernel(
             acc = banks[bank_order[g]]
             for n_part, (m0, j) in enumerate(parts[g]):
                 width = widths[m0]
-                words, n0 = (wdis_sb, j * P) if j * P < LATE_N else (wdis_late, j * P - LATE_N)
                 at = (j - parts[g][0][1]) * QUARTER + m0 - parts[g][0][0]
                 nc.tensor.matmul_mx(
                     out=acc[:, at : at + width],
-                    lhsT=words[:, a, n0 : n0 + P].bitcast(FP8X4),
+                    lhsT=wdis_sb[:, a, j * P : (j + 1) * P].bitcast(FP8X4),
                     lhsT_scale=wdis_plane[:, a * N + j * P : a * N + (j + 1) * P],
                     rhs=z_codes[a, m0].bitcast(FP8X4),
                     rhs_scale=z_planes[a, m0],
@@ -483,7 +482,7 @@ def tile_list_surplus_exchange_slots_kernel(
             squashed = kept([P, width], F32, f"squashed{m0}")
             nc.scalar.activation(squashed[:], total[:], ACT.Tanh)
             nc.vector.tensor_scalar(z_pairs[m0][:, 1, :, 1], squashed[:], gain_sb[:, 1, last : last + 1], None, MULT)
-            woven = placed([P, width, PACK], BF16, f"z1_woven{m0}", TAB_AT + 8 * m0)
+            woven = placed([P, width, PACK], BF16, f"z1_woven{m0}", TURNED_AT + 8 * m0)
             nc.vector.tensor_copy(woven_words(woven, I32), words_of(z_pairs[m0], I32))
             quantize_z(1, m0, width, woven)
         for g in range(len(parts)):

@@ -261,13 +261,15 @@ def tile_list_surplus_exchange_slots_kernel(
             nc.sync.dma_start(tile[:], rows)
             return tile
 
-        def add_turned(terms, total_banks):
+        def add_turned(terms, total_banks, last_blocks=None):
             for n_term, term in enumerate(terms):
                 for half in range(HALVES):
                     for b in range(BLOCKS_PER_BANK):
                         m0 = half * BANK + b * P
+                        late = last_blocks is not None and n_term == 0 and b == BLOCKS_PER_BANK - 1
                         nc.tensor.matmul(
-                            total_banks[half][:, b * P : (b + 1) * P], term[:, m0 : m0 + P], ident[:],
+                            total_banks[half][:, b * P : (b + 1) * P],
+                            last_blocks[:, half, :] if late else term[:, m0 : m0 + P], ident[:],
                             is_transpose=True,
                             start=(n_term == 0 and b == 0),
                             stop=(n_term == len(terms) - 1 and b == BLOCKS_PER_BANK - 1),
@@ -311,7 +313,8 @@ def tile_list_surplus_exchange_slots_kernel(
 
         def bound_tile(i):
             total_banks = pairs[i % 2]
-            add_turned([standing[i]] + pages_of(i), total_banks)
+            sup_page, dem_page = pages_of(i)
+            add_turned([sup_page, standing[i], dem_page], total_banks)
             for half in range(HALVES):
                 nc.scalar.activation(
                     bounded[half][:, :, :, 32 * i : 32 * (i + 1)],
@@ -418,8 +421,12 @@ def tile_list_surplus_exchange_slots_kernel(
         last = PACK - 1
         h2_last = placed([P, S], F32, "h2_last", TAB_AT + 2 * KIB)
         h2_planes.append(demand(PACK + last, h2_last[:], next_acc()))
-        for t in range(2, PACK):
-            standing.append(load_standing(stand_planes[:, t, :], placed([P, T2], F32, f"standing{t}", RAW_AT + 4 * t * KIB)))
+        standing.append(load_standing(stand_planes[:, 2, :], placed([P, T2], F32, "standing2", RAW_AT + 8 * KIB)))
+        last_stand = stand_planes[:, last, :].rearrange("p (h m) -> p h m", h=HALVES)
+        standing.append(placed([P, T2], F32, "standing3", RAW_AT + 12 * KIB))
+        nc.sync.dma_start(
+            standing[-1][:].rearrange("p (h m) -> p h m", h=HALVES)[:, :, : BANK - P], last_stand[:, :, : BANK - P]
+        )
 
         z_pairs = {
             m0: placed([P, 2, width, 2], BF16, f"z1_pairs{m0}", RAW_LATE_AT + 16 * KIB + 8 * m0) for m0, width in CHUNKS
@@ -444,15 +451,17 @@ def tile_list_surplus_exchange_slots_kernel(
                             z_pairs[m0][:, t // 2, :, t % 2], back[:, c0 : c0 + width],
                             ACT.Copy, scale=gain_sb[:, 1, t : t + 1],
                         )
-        add_turned([standing[PACK + last], last_sup], pairs[0])
-        partial = pairs[1]
+        last_blocks = placed([P, HALVES, P], F32, "last_blocks", SPARE_AT + 4 * KIB - 64)
+        nc.sync.dma_start(last_blocks[:], last_stand[:, :, BANK - P :])
+        add_turned([standing[PACK + last], last_sup], pairs[1], last_blocks)
+        partial = pairs[0]
         for half in range(HALVES):
-            turn_back(pairs[0][half], ACT.Copy, [partial[half][:, b * P : (b + 1) * P] for b in range(4)])
+            turn_back(pairs[1][half], ACT.Copy, [partial[half][:, b * P : (b + 1) * P] for b in range(4)])
 
-        wdis_sb = placed([P, R_PASSES, N], U32, "wdis_sb", SPARE_AT - 2 * KIB)
+        wdis_sb = placed([P, R_PASSES, N], U32, "wdis_sb", SPARE_AT - 2 * KIB - 64)
         nc.sync.dma_start(wdis_sb[:].bitcast(I32), wdis_rows)
         out_rows = out.rearrange("(j p) m -> p j m", p=P)
-        bank_order = (7, 0, 1, 2, 3, 4, 5, 6, 7, 0, 1, 2)
+        bank_order = (7, 0, 1, 2, 5, 6, 3, 4, 7, 0, 1, 2)
         parts = [[(0, j), (0, j + 1), (128, j), (128, j + 1)] for j in range(0, 6, 2)]
         parts = parts + [[(256, j), (256, j + 1)] for j in range(0, 6, 2)] + [[(512, j)] for j in range(6)]
         widths = dict(CHUNKS)

from contextlib import ExitStack

import concourse.mybir as mybir
from concourse.masks import make_identity

K, T, S, T2, H, N = 1536, 2048, 512, 1024, 1024, 768
FLOPS = 2 * K * H * S * 2 + 2 * H * N * T2

F32 = mybir.dt.float32
BF16 = mybir.dt.bfloat16
I32 = mybir.dt.int32
U32 = mybir.dt.uint32
U16 = mybir.dt.uint16
U8 = mybir.dt.uint8
FP8X4 = mybir.dt.float8_e4m3fn_x4
FP4X4 = mybir.dt.float4_e2m1fn_x4
MULT = mybir.AluOpType.mult
ADD = mybir.AluOpType.add
ACT = mybir.ActivationFunctionType

P = 128
PACK = 4
K_PASS = P * PACK
K_PASSES = K // K_PASS
R_PASSES = H // K_PASS
BANK = 512
BLOCKS_PER_BANK = BANK // P
HALVES = T2 // BANK
QUARTER = 256
SUP_PAGES = 3
DEM_PAGES = 3
FIRST_COLS = 2 * P
EARLY_COLS = 4 * P
LIVE_ROWS = 100
KIB = 1024
PIECES = (((0, 128),), ((128, 128), (256, 256)))
CHUNKS = ((0, 128), (128, 128), (256, 256), (512, 512))
EARLY_GROUPS = 6

TAB_AT = 0
WOVEN_AT = 26 * KIB
SPARE_AT = 32 * KIB
RAW_AT = 36 * KIB
MID_AT = RAW_AT + 8 * KIB - 1536
RAW_LATE_AT = RAW_AT + 24 * KIB
TURNED_AT = RAW_LATE_AT + 24 * KIB


def tile_list_surplus_exchange_slots_kernel(
    tc, tab_words, tab_scales, offs, offs2, offs3, wsup_words, wsup_scales, wdem,
    wg1, wg2, stand, gain, wdis_words, wdis_scales, out,
):
    nc = tc.nc
    with ExitStack() as ctx:
        keep = ctx.enter_context(tc.tile_pool(name="keep", bufs=1))
        ring = ctx.enter_context(tc.tile_pool(name="ring", bufs=1))
        shared = ctx.enter_context(tc.tile_pool(name="shared", bufs=1))
        psum = ctx.enter_context(tc.psum_pool(name="psum", bufs=1))

        def placed(shape, dtype, name, offset):
            return shared.tile(shape, dtype, name=name, offset=offset, align_bytes=64)

        def kept(shape, dtype, name):
            return keep.tile(shape, dtype, name=name, align_bytes=64)

        def load_list(source, name):
            tile = keep.tile([P, S // 16], U16, name=name)
            nc.sync.dma_start(tile[:], source)
            return tile

        def zero(tile, engine):
            engine.memset(tile[:].bitcast(I32), 0)

        def load_scale_rows(plane, source, cols, queue):
            passes = source.shape[0]
            for quad in range(4):
                queue.dma_start(
                    plane[32 * quad : 32 * quad + 4, :].rearrange("r (a c) -> r a c", a=passes).bitcast(I32),
                    source[:, 4 * quad : 4 * quad + 4, cols].rearrange("a r c -> r a c").bitcast(I32),
                )

        tab_plane = placed([P, T], U8, "tab_plane", MID_AT - 64)
        zero(tab_plane, nc.gpsimd)
        wsup_plane_early = placed([P, K_PASSES * EARLY_COLS], U8, "wsup_plane_early", WOVEN_AT + 4 * KIB)
        zero(wsup_plane_early, nc.gpsimd)
        lot_planes = [kept([P, S], U8, f"lot_plane{a}") for a in range(K_PASSES)]
        for a in range(1, K_PASSES):
            zero(lot_planes[a], nc.vector)
        sup_pages = [keep.tile([P, T2], F32, name=f"sup_page{i}") for i in range(SUP_PAGES)]
        for page in sup_pages:
            zero(page, nc.vector)

        tab_tiles = []

        def load_tab(a):
            tile = placed([P, T], U32, f"tab{a}", TAB_AT + a * 4 * T)
            nc.sync.dma_start(tile[:].bitcast(I32), tab_words[a].rearrange("p t i -> p (t i)").bitcast(I32))
            tab_tiles.append(tile)

        def load_wsup(tile, c0, c1):
            nc.sync.dma_start(
                tile[:].bitcast(I32), wsup_words.rearrange("a p c -> p a c")[:, :, 2 * c0 : 2 * c1].bitcast(I32)
            )
            return tile

        load_tab(0)
        lot_list = load_list(offs, "lot_list")
        for quad in range(4):
            (nc.sync if quad < 2 else nc.scalar).dma_start(
                tab_plane[32 * quad : 32 * quad + 4 * K_PASSES, :].bitcast(I32),
                tab_scales[:, 4 * quad : 4 * quad + 4, :].bitcast(I32),
            )
        load_tab(1)
        wsup_first = load_wsup(placed([P, K_PASSES, 2 * FIRST_COLS], U8, "wsup_first", WOVEN_AT + 2 * KIB - 768), 0, FIRST_COLS)
        load_tab(2)
        sup_list = load_list(offs2, "sup_list")
        dem_list = load_list(offs3, "dem_list")
        load_scale_rows(wsup_plane_early, wsup_scales, slice(0, EARLY_COLS), nc.gpsimd)

        lot_words = [kept([P, S], U32, f"lot_words{a}") for a in range(K_PASSES)]
        nc.vector.tensor_copy(lot_words[0][:], tab_tiles[0][:].indirect(lot_list[:]))
        nc.vector.tensor_copy(lot_planes[0][:], tab_plane[:].indirect(lot_list[:]))
        for a in range(1, K_PASSES):
            nc.sync.dma_start(
                lot_planes[a][:LIVE_ROWS, :].bitcast(I32), lot_planes[0][4 * a : 4 * a + LIVE_ROWS, :].bitcast(I32)
            )
        wg1_sb = placed([P, S], F32, "wg1_sb", MID_AT - 2 * KIB)
        nc.sync.dma_start(wg1_sb[:], wg1)
        wsup_mid = load_wsup(placed([P, K_PASSES, 2 * (K_PASS - FIRST_COLS)], U8, "wsup_mid", MID_AT), FIRST_COLS, K_PASS)

        def span(piece):
            return piece[0][0], piece[-1][0] + piece[-1][1]

        nc.vector.tensor_copy(lot_words[1][:], tab_tiles[1][:].indirect(lot_list[:]))
        for piece in PIECES:
            j0, j1 = span(piece)
            nc.vector.tensor_copy(lot_words[2][:, j0:j1], tab_tiles[2][:].indirect(lot_list[:, j0 // 16 : j1 // 16]))

        late_cols = H - EARLY_COLS
        wsup_plane_late = placed([P, K_PASSES * late_cols], U8, "wsup_plane_late", TAB_AT + 8 * KIB)
        zero(wsup_plane_late, nc.gpsimd)
        dem_pages = []

        def zeroed_page(name, offset):
            page = placed([P, T2], F32, name, offset)
            nc.gpsimd.memset(page[:], 0.0)
            dem_pages.append(page)

        zeroed_page("dem_page0", TAB_AT + 14 * KIB)
        zeroed_page("dem_page1", TAB_AT + 18 * KIB)
        ident = keep.tile([P, P], F32, name="ident")
        make_identity(nc, ident[:])
        zeroed_page("dem_page2", TAB_AT + 22 * KIB)
        wdis_plane = placed([P, R_PASSES * N], U8, "wdis_plane", TAB_AT + 12 * KIB)
        zero(wdis_plane, nc.gpsimd)

        banks = [psum.tile([P, BANK], F32, name=f"bank{i}") for i in range(8)]
        pairs = (banks[3:5], banks[5:7])
        acc_turn = []

        def next_acc():
            acc_turn.append(None)
            return banks[(len(acc_turn) + 1) % 3]

        def score_tile():
            return ring.tile([P, S], F32, name="scores", tag="scores", bufs=12)

        def supply(i, h1, acc, piece=((0, S),)):
            words, c0 = (wsup_first, i * P) if i * P < FIRST_COLS else (wsup_mid, i * P - FIRST_COLS)
            j0, j1 = span(piece)
            order = (0, 1, 2) if j1 == P else (2, 0, 1)
            for a in order:
                for n_part, (j, width) in enumerate(piece):
                    nc.tensor.matmul_mx(
                        out=acc[:, j - j0 : j - j0 + width],
                        lhsT=words[:, a, 2 * c0 : 2 * (c0 + P)].bitcast(FP4X4),
                        lhsT_scale=wsup_plane_early[:, a * EARLY_COLS + i * P : a * EARLY_COLS + (i + 1) * P],
                        rhs=lot_words[a][:, j : j + width].bitcast(FP8X4),
                        rhs_scale=lot_planes[a][:, j : j + width],
                        start=(a == order[0] and n_part == 0),
                        stop=(a == order[-1] and n_part == len(piece) - 1),
                    )
            nc.scalar.copy(h1[:, j0:j1], acc[:, : j1 - j0])
            return h1

        def supply_turned(words, turned, blocks, accs):
            s0 = K_PASS - EARLY_COLS
            for jb, acc in zip(blocks, accs):
                for a in range(K_PASSES):
                    nc.tensor.matmul_mx(
                        out=acc[:],
                        lhsT=lot_words[a][:, jb * P : (jb + 1) * P].bitcast(FP8X4),
                        lhsT_scale=lot_planes[a][:, jb * P : (jb + 1) * P],
                        rhs=words[:, a, :].bitcast(FP4X4),
                        rhs_scale=wsup_plane_late[:, a * late_cols + s0 : a * late_cols + s0 + BANK],
                        start=(a == 0),
                        stop=(a == K_PASSES - 1),
                    )
                nc.scalar.copy(turned[:, jb], acc[:].rearrange("j (p t) -> j t p", t=PACK))

        def supply_plane(turned, t, h1):
            acc = next_acc()
            for jb in range(S // P):
                nc.tensor.transpose(acc[:, jb * P : (jb + 1) * P], turned[:, jb, t, :], ident[:])
            nc.scalar.copy(h1, acc[:])
            return h1

        wdem_codes = {}
        wdem_planes = {}

        def load_wdem(a, c0, width, offset):
            raw = placed([P, PACK, width], F32, f"wdem_raw{a}_{c0}", offset)
            nc.sync.dma_start(
                raw[:], wdem[a * K_PASS : (a + 1) * K_PASS, c0 : c0 + width].rearrange("(p j) c -> p j c", j=PACK)
            )
            return raw

        def quantize_wdem(a, c0, raw, woven):
            width = raw.shape[2]
            if c0 < K_PASS:
                nc.scalar.copy(
                    woven[:].rearrange("p (c i) j -> p c j i", i=4),
                    raw[:].rearrange("p j (c i) -> p c j i", i=4),
                )
            else:
                nc.scalar.copy(
                    woven[:].rearrange("p (t q) j -> p q j t", t=PACK),
                    raw[:].rearrange("p j (q t) -> p q j t", t=PACK),
                )
            codes = kept([P, width], U32, f"wdem_codes{a}_{c0}")
            plane = kept([P, width], U8, f"wdem_plane{a}_{c0}")
            nc.vector.quantize_mx(
                out=codes[:].bitcast(FP8X4), scales=plane[:], in_=woven[:].rearrange("p c j -> p (c j)")
            )
            for c in range(0, width, P):
                wdem_codes[a, (c0 + c) // P] = codes[:, c : c + P]
                wdem_planes[a, (c0 + c) // P] = plane[:, c : c + P]

        def demand(i, h2, acc):
            for a in range(K_PASSES):
                nc.tensor.matmul_mx(
                    out=acc[:],
                    lhsT=wdem_codes[a, i].bitcast(FP8X4),
                    lhsT_scale=wdem_planes[a, i],
                    rhs=lot_words[a][:].bitcast(FP8X4),
                    rhs_scale=lot_planes[a][:],
                    start=(a == 0),
                    stop=(a == K_PASSES - 1),
                )
            nc.scalar.activation(h2, acc[:], ACT.Copy, scale=-1.0)
            return h2

        def place(page, slots, scores, weights, j0=0, j1=S):
            nc.vector.tensor_tensor(
                page[:].indirect(slots[:, j0 // 16 : j1 // 16]), scores[:, j0:j1], weights[:, j0:j1], MULT
            )

        def load_standing(rows, tile=None):
            if tile is None:
                tile = ring.tile([P, T2], F32, name="standing", tag="standing", bufs=4)
            nc.sync.dma_start(tile[:], rows)
            return tile

        def add_turned(terms, total_banks, last_blocks=None):
            for n_term, term in enumerate(terms):
                for half in range(HALVES):
                    for b in range(BLOCKS_PER_BANK):
                        m0 = half * BANK + b * P
                        late = last_blocks is not None and n_term == 0 and b == BLOCKS_PER_BANK - 1
                        nc.tensor.matmul(
                            total_banks[half][:, b * P : (b + 1) * P],
                            last_blocks[:, half, :] if late else term[:, m0 : m0 + P], ident[:],
                            is_transpose=True,
                            start=(n_term == 0 and b == 0),
                            stop=(n_term == len(terms) - 1 and b == BLOCKS_PER_BANK - 1),
                        )

        def turn_back(total, func, targets, turned=None):
            if turned is None:
                turned = ring.tile([P, BANK], F32, name="turned_sum", tag="turned_sum", bufs=3)
            nc.scalar.activation(turned[:], total[:], func)
            for b in range(BLOCKS_PER_BANK):
                nc.tensor.transpose(targets[b], turned[:, b * P : (b + 1) * P], ident[:])

        z_codes = {}
        z_planes = {}

        def quantize_z(a, m0, width, woven, codes=None):
            if codes is None:
                codes = kept([P, width], U32, f"z_codes{a}_{m0}")
            plane = kept([P, width], U8, f"z_plane{a}_{m0}")
            nc.vector.quantize_mx(
                out=codes[:].bitcast(FP8X4), scales=plane[:], in_=woven[:].rearrange("p m t -> p (m t)")
            )
            for c0, cw in CHUNKS:
                if m0 <= c0 < m0 + width:
                    z_codes[a, c0] = codes[:, c0 - m0 : c0 - m0 + cw]
                    z_planes[a, c0] = plane[:, c0 - m0 : c0 - m0 + cw]

        def words_of(pair_tile, dtype):
            return pair_tile[:].rearrange("p u m e -> p (u m e)").bitcast(dtype).rearrange("p (u m) -> p m u", u=2)

        def woven_words(woven, dtype):
            return woven[:].rearrange("p m t -> p (m t)").bitcast(dtype).rearrange("p (m u) -> p m u", u=2)

        bounded = [
            placed([P, BLOCKS_PER_BANK, PACK, P], F32, f"bounded{half}", RAW_AT + (16 - 8 * half) * KIB)
            for half in range(HALVES)
        ]

        def pages_of(i):
            return [sup_pages[i % SUP_PAGES], dem_pages[i % DEM_PAGES]]

        def bound_tile(i):
            total_banks = pairs[i % 2]
            sup_page, dem_page = pages_of(i)
            add_turned([sup_page, standing[i], dem_page], total_banks)
            for half in range(HALVES):
                nc.scalar.activation(
                    bounded[half][:, :, :, 32 * i : 32 * (i + 1)],
                    total_banks[half][:].rearrange("m (b q t) -> m b t q", b=BLOCKS_PER_BANK, t=PACK),
                    ACT.Tanh,
                )

        first_scores = [score_tile()[:] for i in range(2)]
        for n_piece, piece in enumerate(PIECES):
            for i in range(2):
                supply(i, first_scores[i], pairs[n_piece][i], piece)
                place(sup_pages[i], sup_list, first_scores[i], wg1_sb[:], *span(piece))

        def quantize_quarter(quarter, passes, raw_at, woven_at):
            raws = [load_wdem(a, quarter * QUARTER, QUARTER, at) for a, at in zip(passes, raw_at)]
            for a, raw in zip(passes, raws):
                woven = placed([P, QUARTER, PACK], BF16, f"woven{a}_{quarter}", woven_at + 2 * a * KIB)
                quantize_wdem(a, quarter * QUARTER, raw, woven)
            return raws[-1][:].rearrange("p j c -> p (j c)")[:, :S]

        late_raws = []

        def quantize_late(a):
            late_raws.append(load_wdem(a, K_PASS, K_PASS, RAW_LATE_AT + 8 * a * KIB))
            woven = ring.tile([P, K_PASS, PACK], BF16, name="woven", tag="woven", bufs=3, align_bytes=64)
            quantize_wdem(a, K_PASS, late_raws[a], woven)

        place(sup_pages[2], sup_list, supply(2, quantize_quarter(0, (0, 1, 2), (RAW_AT + 8 * KIB, TAB_AT, TAB_AT + 4 * KIB), WOVEN_AT), next_acc()), wg1_sb[:])
        wg2_sb = keep.tile([P, S], F32, name="wg2_sb")
        nc.sync.dma_start(wg2_sb[:], wg2)
        quantize_quarter(1, (0, 1), (RAW_AT + 16 * KIB, RAW_AT + 20 * KIB), SPARE_AT)
        load_scale_rows(wsup_plane_late, wsup_scales, slice(EARLY_COLS, H), nc.sync)
        wsup_late = load_wsup(kept([P, K_PASSES, 2 * K_PASS], U8, "wsup_late"), K_PASS, H)
        sup_turned = placed([P, S // P, PACK, P], F32, "turned", TURNED_AT)
        standing = [load_standing(stand[0:P, :])]
        for i in range(2):
            place(dem_pages[i], dem_list, demand(i, score_tile()[:], banks[i]), wg2_sb[:])
        supply_turned(wsup_late, sup_turned, range(4), pairs[1] + banks[:2])
        h1_tile3 = supply(3, quantize_quarter(1, (2,), (RAW_AT,), WOVEN_AT), banks[7])
        bound_tile(0)
        place(sup_pages[0], sup_list, h1_tile3, wg1_sb[:])
        quantize_late(0)
        place(dem_pages[2], dem_list, demand(2, late_raws[0][:, 0, :], next_acc()), wg2_sb[:])
        h2_tile3 = demand(3, late_raws[0][:, 1, :], next_acc())
        place(dem_pages[0], dem_list, h2_tile3, wg2_sb[:])
        standing.append(load_standing(stand[P : 2 * P, :]))
        bound_tile(1)
        for a in range(1, K_PASSES):
            quantize_late(a)
        standing.append(load_standing(stand[2 * P : 3 * P, :]))
        standing.append(load_standing(stand[3 * P : 4 * P, :]))
        h1_planes = [supply_plane(sup_turned, 0, late_raws[2][:, 1, :])]
        h1_planes = h1_planes + [supply_plane(sup_turned, t, score_tile()[:]) for t in range(1, PACK - 1)]

        wg1_dealt = []
        wg2_dealt = []

        def load_dealt(t):
            for dealt, source, name in ((wg1_dealt, wg1, "wg1"), (wg2_dealt, wg2, "wg2")):
                tile = keep.tile([P, S], F32, name=f"{name}_dealt{t}")
                for rep in range(P // 32):
                    nc.sync.dma_start(
                        tile[32 * rep : 32 * (rep + 1)], source.rearrange("(q t) j -> q t j", t=PACK)[:, t, :]
                    )
                dealt.append(tile)

        def place_plane(t):
            sup_page, dem_page = pages_of(PACK + t)
            place(sup_page, sup_list, h1_planes[t], wg1_dealt[t][:])
            place(dem_page, dem_list, h2_planes[t], wg2_dealt[t][:])

        bound_tile(2)
        bound_tile(3)
        h2_planes = [demand(PACK + t, score_tile()[:], next_acc()) for t in range(PACK - 1)]
        for t in range(PACK - 1):
            load_dealt(t)
        gain_sb = keep.tile([P, R_PASSES, PACK], F32, name="gain_sb")
        nc.sync.dma_start(gain_sb[:], gain.rearrange("(a p t) -> p a t", p=P, t=PACK))
        stand_planes = stand[K_PASS:, :].rearrange("(p t) m -> p t m", t=PACK)
        standing.append(load_standing(stand_planes[:, 0, :]))
        standing.append(load_standing(stand_planes[:, 1, :], placed([P, T2], F32, "standing1", TAB_AT)))
        load_dealt(3)
        wdis_rows = wdis_words.rearrange("a p c i -> p a (c i)").bitcast(I32)
        load_scale_rows(wdis_plane, wdis_scales, slice(0, N), nc.sync)

        for t in range(PACK - 1):
            place_plane(t)

        z0_banks = (7, 0, 1, 2, 7, 0, 5, 6)
        z0_woven = []
        for half in range(HALVES):
            rows = placed([P, 2, BANK, 2], BF16, f"z0_pairs{half}", RAW_LATE_AT + 4 * half * KIB)
            for t in range(PACK):
                back = banks[z0_banks[half * PACK + t]]
                for b in range(BLOCKS_PER_BANK):
                    nc.tensor.transpose(back[:, b * P : (b + 1) * P], bounded[half][:, b, t, :], ident[:])
                nc.scalar.activation(rows[:, t // 2, :, t % 2], back[:], ACT.Copy, scale=gain_sb[:, 0, t : t + 1])
            woven = placed([P, BANK, PACK], BF16, f"z0_woven{half}", RAW_LATE_AT + (8 + 4 * half) * KIB)
            nc.scalar.copy(woven_words(woven, U32), words_of(rows, U32))
            z0_woven.append(woven)
            if half == 0:
                h1_last = placed([P, S], F32, "h1_last", RAW_LATE_AT)
                h1_planes.append(supply_plane(sup_turned, PACK - 1, h1_last[:]))
        last = PACK - 1
        h2_last = placed([P, S], F32, "h2_last", TAB_AT + 2 * KIB)
        h2_planes.append(demand(PACK + last, h2_last[:], next_acc()))
        standing.append(load_standing(stand_planes[:, 2, :], placed([P, T2], F32, "standing2", RAW_AT + 8 * KIB)))
        last_stand = stand_planes[:, last, :].rearrange("p (h m) -> p h m", h=HALVES)
        standing.append(placed([P, T2], F32, "standing3", RAW_AT + 12 * KIB))
        nc.sync.dma_start(
            standing[-1][:].rearrange("p (h m) -> p h m", h=HALVES)[:, :, : BANK - P], last_stand[:, :, : BANK - P]
        )

        z_pairs = {
            m0: placed([P, 2, width, 2], BF16, f"z1_pairs{m0}", RAW_LATE_AT + 16 * KIB + 8 * m0) for m0, width in CHUNKS
        }
        last_sup, last_page = pages_of(PACK + last)
        for t in range(last):
            total_banks = pairs[t % 2]
            add_turned([standing[PACK + t]] + pages_of(PACK + t), total_banks)
            if t == 0:
                place(last_sup, sup_list, h1_planes[last], wg1_dealt[last][:])
            else:
                codes = placed([P, BANK], U32, f"z0_codes{t - 1}", (TAB_AT, RAW_AT + 8 * KIB)[t - 1])
                quantize_z(0, (t - 1) * BANK, BANK, z0_woven[t - 1], codes)
            for half in range(HALVES):
                back = banks[((1, 2), (7, 0), (1, 2))[t][half]]
                own = placed([P, BANK], F32, f"plane1_tanh{half}", SPARE_AT + 2 * half * KIB) if t == 1 else None
                turn_back(total_banks[half], ACT.Tanh, [back[:, b * P : (b + 1) * P] for b in range(4)], own)
                for m0, width in CHUNKS:
                    if m0 // BANK == half:
                        c0 = m0 % BANK
                        nc.scalar.activation(
                            z_pairs[m0][:, t // 2, :, t % 2], back[:, c0 : c0 + width],
                            ACT.Copy, scale=gain_sb[:, 1, t : t + 1],
                        )
        last_blocks = placed([P, HALVES, P], F32, "last_blocks", SPARE_AT + 4 * KIB - 64)
        nc.sync.dma_start(last_blocks[:], last_stand[:, :, BANK - P :])
        add_turned([standing[PACK + last], last_sup], pairs[1], last_blocks)
        partial = pairs[0]
        for half in range(HALVES):
            turn_back(pairs[1][half], ACT.Copy, [partial[half][:, b * P : (b + 1) * P] for b in range(4)])

        wdis_sb = placed([P, R_PASSES, N], U32, "wdis_sb", SPARE_AT - 2 * KIB - 64)
        nc.sync.dma_start(wdis_sb[:].bitcast(I32), wdis_rows)
        out_rows = out.rearrange("(j p) m -> p j m", p=P)
        bank_order = (7, 0, 1, 2, 5, 6, 3, 4, 7, 0, 1, 2)
        parts = [[(0, j), (0, j + 1), (128, j), (128, j + 1)] for j in range(0, 6, 2)]
        parts = parts + [[(256, j), (256, j + 1)] for j in range(0, 6, 2)] + [[(512, j)] for j in range(6)]
        widths = dict(CHUNKS)

        def dispatch_pass(a, g):
            acc = banks[bank_order[g]]
            for n_part, (m0, j) in enumerate(parts[g]):
                width = widths[m0]
                at = (j - parts[g][0][1]) * QUARTER + m0 - parts[g][0][0]
                nc.tensor.matmul_mx(
                    out=acc[:, at : at + width],
                    lhsT=wdis_sb[:, a, j * P : (j + 1) * P].bitcast(FP8X4),
                    lhsT_scale=wdis_plane[:, a * N + j * P : a * N + (j + 1) * P],
                    rhs=z_codes[a, m0].bitcast(FP8X4),
                    rhs_scale=z_planes[a, m0],
                    start=(a == 0 and n_part == 0),
                    stop=(a == R_PASSES - 1 and n_part == len(parts[g]) - 1),
                )

        for g in range(EARLY_GROUPS):
            dispatch_pass(0, g)
        place(last_page, dem_list, h2_planes[last], wg2_dealt[last][:])
        for m0, width in CHUNKS:
            half, c0 = divmod(m0, BANK)
            total = kept([P, width], F32, f"total{m0}")
            nc.vector.tensor_tensor(total[:], partial[half][:, c0 : c0 + width], last_page[:, m0 : m0 + width], ADD)
            squashed = kept([P, width], F32, f"squashed{m0}")
            nc.scalar.activation(squashed[:], total[:], ACT.Tanh)
            nc.vector.tensor_scalar(z_pairs[m0][:, 1, :, 1], squashed[:], gain_sb[:, 1, last : last + 1], None, MULT)
            woven = placed([P, width, PACK], BF16, f"z1_woven{m0}", TURNED_AT + 8 * m0)
            nc.vector.tensor_copy(woven_words(woven, I32), words_of(z_pairs[m0], I32))
            quantize_z(1, m0, width, woven)
        for g in range(len(parts)):
            if g >= EARLY_GROUPS:
                dispatch_pass(0, g)
            dispatch_pass(1, g)
            m0, j0 = parts[g][0]
            if g < EARLY_GROUPS:
                result = score_tile()[:]
            else:
                if j0 % 2 == 0:
                    both = placed([P, 2, BANK], F32, f"result{g}", RAW_AT + (0, 16, 20)[j0 // 2] * KIB)
                result = both[:, j0 % 2, :]
            if g in (7, 9, 11):
                nc.vector.tensor_copy(result, banks[bank_order[g]][:])
            else:
                nc.scalar.copy(result, banks[bank_order[g]][:])
            tiles = parts[g][-1][1] - j0 + 1
            if g < EARLY_GROUPS:
                nc.sync.dma_start(
                    out_rows[:, j0 : j0 + tiles, m0 : m0 + BANK // tiles], result.rearrange("p (j m) -> p j m", j=tiles)
                )
            elif j0 % 2 == 1:
                nc.sync.dma_start(out_rows[:, j0 - 1 : j0 + 1, m0 : m0 + BANK], both[:])
